import numpy as np
import ml_dtypes


def mxq(x, axis, fmt="e4m3"):
    dtype, down = {"e4m3": (ml_dtypes.float8_e4m3fn, 7), "e5m2": (ml_dtypes.float8_e5m2, 14)}[fmt]
    v = np.moveaxis(np.asarray(x, np.float32).astype(ml_dtypes.bfloat16).astype(np.float64), axis, -1)
    blocks = v.reshape(v.shape[:-1] + (-1, 32))
    amax = np.abs(blocks).max(-1, keepdims=True)
    byte = np.maximum(np.where(amax > 0, np.frexp(amax)[1] - 1 + 127, 0) - down, 1)
    scale = np.exp2(byte - 127.0)
    codes = (blocks / scale).astype(np.float32).astype(dtype).astype(np.float64)
    return np.moveaxis((codes * scale).reshape(v.shape), -1, axis)


WIDE = False


def mx_kscale(k):
    if not WIDE:
        return np.ones(k)
    levels = np.array([10, -10, 5, -5, 0])
    if k % 512:
        return np.exp2(np.random.permutation(np.resize(levels, k // 32))).repeat(32)
    a = np.empty((k // 512, 16))
    for p in range(k // 512):
        a[p, :8] = np.random.permutation(np.resize(levels, 8))
        for g in range(8):
            far = levels[np.abs(levels - a[p, g]) >= 10]
            a[p, g + 8] = far[np.random.randint(len(far))]
    return np.exp2(a.ravel()).repeat(32)


def f64(x):
    return np.asarray(x).astype(np.float64)


def striped(idx):
    return np.tile(idx.reshape(-1, 16).T, (8, 1)).astype(np.uint16)


def unstriped(offs):
    return offs[:16].T.reshape(-1).astype(np.int64)


def pack_weight(w):
    k, n = w.shape
    w = f64(np.asarray(w, np.float32).astype(ml_dtypes.bfloat16)).reshape(k // 32, 32, n)
    amax = np.abs(w).max(1)
    byte = np.clip(np.where(amax > 0, np.frexp(amax)[1] - 1 + 127 - 7, 1), 1, 254)
    scaled = (w * np.exp2(127.0 - byte)[:, None, :]).reshape(k, n).astype(np.float32)
    words = np.ascontiguousarray(scaled.reshape(k // 512, 128, 4, n).transpose(0, 1, 3, 2)).astype(ml_dtypes.float8_e4m3fn).view(np.uint8)
    return words, np.ascontiguousarray(byte.astype(np.uint8).reshape(k // 512, 16, n))


def unpack_weight(words, scales):
    g, p, n, _ = words.shape
    vals = np.ascontiguousarray(words).view(ml_dtypes.float8_e4m3fn).astype(np.float64) * np.repeat(np.exp2(scales.astype(np.float64) - 127.0), 8, axis=1)[..., None]
    return vals.transpose(0, 1, 3, 2).reshape(g * 512, n)


K, T, S, H, V, W, G, U = 1024, 1024, 512, 512, 256, 2048, 1024, 512


def setup_inputs():
    n = np.random.standard_normal
    s = mx_kscale(K)[:, None]
    u = mx_kscale(H)
    packed_xT = pack_weight(n((K, T)) * s)
    packed_eT = pack_weight(n((H, W)) / np.sqrt(H) / u[:, None])
    packed_dT = pack_weight(n((H, G)) / np.sqrt(H) / u[:, None])
    return {
        "x_words": packed_xT[0],
        "x_scales": packed_xT[1],
        "w1": (n((K, H)) / np.sqrt(K) / s * u).astype(np.float32),
        "e_words": packed_eT[0],
        "e_scales": packed_eT[1],
        "d_words": packed_dT[0],
        "d_scales": packed_dT[1],
        "offs": striped(np.random.permutation(T)[:S]),
        "bank": striped(np.random.permutation(W)[:U]),
        "qry": striped(np.random.permutation(G)[:V]),
    }


def reference(x_words, x_scales, w1, e_words, e_scales, d_words, d_scales, offs, bank, qry):
    xq = unpack_weight(x_words, x_scales)[:, unstriped(offs)]
    h = mxq(f64(w1), 0, "e4m3").T @ xq
    hq = mxq(h, 0, "e4m3")
    d_qry = unpack_weight(d_words, d_scales)[:, unstriped(qry)]
    ss = hq.T @ d_qry
    e_bank = unpack_weight(e_words, e_scales)[:, unstriped(bank)]
    y = hq.T @ e_bank
    top = y.max(axis=1, keepdims=True)
    ex = np.exp(y - top)
    total = ex.sum(axis=1, keepdims=True)
    return np.exp(ss - top) / total

@@ -1,0 +1,230 @@
+from contextlib import ExitStack
+
+import concourse.mybir as mybir
+
+K, T, S, H, V, W, G, U = 1024, 1024, 512, 512, 256, 2048, 1024, 512
+FLOPS = 2 * (K * H * S + H * S * V + H * S * U)
+
+F32 = mybir.dt.float32
+BF16 = mybir.dt.bfloat16
+I32 = mybir.dt.int32
+U32 = mybir.dt.uint32
+U16 = mybir.dt.uint16
+U8 = mybir.dt.uint8
+FP8X4 = mybir.dt.float8_e4m3fn_x4
+ACT = mybir.ActivationFunctionType
+ALU = mybir.AluOpType
+AX = mybir.AxisListType
+
+P = 128
+PACK = 4
+PASSES = K // (P * PACK)
+TILES = S // P
+E_ROW = 8
+D_ROW = 12
+
+
+def tile_picked_yqbn_norm_p_kernel(
+    tc, x_words, x_scales, w1, e_words, e_scales, d_words, d_scales, offs, bank, qry, out
+):
+    nc = tc.nc
+    with ExitStack() as ctx:
+        keep = ctx.enter_context(tc.tile_pool(name="keep", bufs=1))
+        psum_h = ctx.enter_context(tc.psum_pool(name="psum_h", bufs=2))
+        psum_y = ctx.enter_context(tc.psum_pool(name="psum_y", bufs=4))
+        psum_s = ctx.enter_context(tc.psum_pool(name="psum_s", bufs=2))
+
+        def sb(name, shape, dtype):
+            return keep.tile(shape, dtype, name=name, align_bytes=64)
+
+        offs_t = sb("offs_t", [P, S // 16], U16)
+        bank_t = sb("bank_t", [P, U // 16], U16)
+        qry_t = sb("qry_t", [P, V // 16], U16)
+        stage = ctx.enter_context(tc.tile_pool(name="stage", bufs=1))
+
+        def at(name, offset, shape, dtype):
+            return stage.tile(shape, dtype, name=name, offset=offset, align_bytes=64)
+
+        half = H // 2
+        kb = 1024
+        es_win = sb("es_win", [P, W], U8)
+        warm = at("warm", 0, [P, 10 * kb // 4], F32)
+        x0_hold = at("x0_hold", 10 * kb, [P, 9 * kb // 4], U32)
+        w0a_hold = at("w0a_hold", 19 * kb, [P, 12 * kb // 4], F32)
+        x0_win = x0_hold[:, 0:T]
+        w0a = w0a_hold[:, 0 : PACK * half].rearrange("p (j i) -> p j i", j=PACK)
+
+        nc.vector.memset(es_win[:].bitcast(I32), 0)
+        nc.vector.memset(warm[:, 0:8], 0.0)
+        warm_out = sb("warm_out", [P, 8], F32)
+        nc.scalar.activation(warm_out[:], warm[:, 0:8], ACT.Exp)
+
+        def load_w(raw, rows):
+            nc.sync.dma_start(out=raw, in_=rows.rearrange("(p j) i -> p j i", j=PACK))
+
+        def load_words(win, words):
+            nc.sync.dma_start(out=win.bitcast(I32), in_=words.rearrange("p n t -> p (n t)").bitcast(I32))
+
+        def load_scales(queue, win, row, scales, q):
+            n = scales.shape[0] * 4
+            queue.dma_start(
+                out=win[32 * q + row : 32 * q + row + n, :].bitcast(I32),
+                in_=scales[:, 4 * q : 4 * q + 4, :].bitcast(I32),
+            )
+
+        w_bf = [sb("w_bf%d" % o, [P, PACK, P, PACK], BF16) for o in range(PASSES)]
+        w_codes = [sb("w_codes%d" % o, [P, H], U32) for o in range(PASSES)]
+        w_sc = [sb("w_sc%d" % o, [P, H], U8) for o in range(PASSES)]
+
+        def weave_w(copy, raw, o, c):
+            src = raw.rearrange("p j (m t) -> p m t j", t=PACK)
+            dst = w_bf[o][:, :, c * 64 : (c + 1) * 64, :].rearrange("p t m j -> p m t j")
+            copy(dst, src)
+
+        def quant_w(o):
+            nc.vector.quantize_mx(
+                out=w_codes[o][:].bitcast(FP8X4), scales=w_sc[o][:], in_=w_bf[o][:].rearrange("p t m j -> p (t m j)")
+            )
+
+        xs_g = sb("xs_g", [P, S], U8)
+        es_g = sb("es_g", [P, U], U8)
+        ds_g = sb("ds_g", [P, V], U8)
+        x0_g = sb("x0_g", [P, S], U32)
+        x1_g = [sb("x1_g%d" % t, [P, P], U32) for t in range(TILES)]
+        e_g = sb("e_g", [P, U], U32)
+        d_g = sb("d_g", [P, V], U32)
+
+        nc.sync.dma_start(offs_t[:], offs)
+        nc.sync.dma_start(bank_t[:], bank)
+        nc.sync.dma_start(qry_t[:], qry)
+        load_words(x0_win, x_words[0])
+        load_w(w0a, w1[0:512, 0:half])
+        for q in range(4):
+            load_scales(nc.sync, es_win, E_ROW, e_scales, q)
+
+        w0b = at("w0b", 0, [P, PACK, half], F32)
+        w1a = at("w1a", 4 * kb, [P, PACK, half], F32)
+        xs_win = at("xs_win", 8 * kb, [P, T], U8)
+        load_w(w0b[:], w1[0:512, half:H])
+        load_w(w1a[:], w1[512:1024, 0:half])
+        nc.vector.memset(xs_win[:].bitcast(I32), 0)
+        for q in range(4):
+            load_scales(nc.sync, xs_win, 0, x_scales, q)
+
+        nc.vector.tensor_copy(x0_g[:], x0_win.indirect(offs_t[:]))
+        w1b = at("w1b", 10 * kb, [P, PACK, half], F32)
+        x1_win = at("x1_win", 14 * kb, [P, T], U32)
+        ds_win = at("ds_win", 18 * kb, [P, G], U8)
+        load_w(w1b[:], w1[512:1024, half:H])
+        load_words(x1_win[:], x_words[1])
+        nc.vector.memset(ds_win[:].bitcast(I32), 0)
+        for q in range(4):
+            load_scales(nc.sync, ds_win, D_ROW, d_scales, q)
+
+        weave_w(nc.scalar.copy, w0a, 0, 0)
+        ew_win = at("ew_win", 23 * kb, [P, W], U32)
+        dw_win = at("dw_win", 19 * kb, [P, G], U32)
+        load_words(ew_win[:], e_words[0])
+        load_words(dw_win[:], d_words[0])
+
+        nc.vector.tensor_copy(es_g[:], es_win[:].indirect(bank_t[:]))
+        weave_w(nc.vector.tensor_copy, w0b[:], 0, 1)
+        quant_w(0)
+        nc.vector.tensor_copy(xs_g[:], xs_win[:].indirect(offs_t[:]))
+        warm_ps = psum_y.tile([P, U], F32, name="y_ps")
+        for j in range(3):
+            nc.tensor.matmul_mx(
+                out=warm_ps[:], lhsT=w_codes[0][:, j * P : (j + 1) * P].bitcast(FP8X4),
+                lhsT_scale=w_sc[0][:, j * P : (j + 1) * P],
+                rhs=x0_g[:].bitcast(FP8X4), rhs_scale=xs_g[:], start=True, stop=True,
+            )
+        weave_w(nc.scalar.copy, w1a[:], 1, 0)
+        weave_w(nc.vector.tensor_copy, w1b[:], 1, 1)
+        quant_w(1)
+        for t in range(TILES):
+            nc.vector.tensor_copy(x1_g[t][:], x1_win[:].indirect(offs_t[:, 8 * t : 8 * t + 8]))
+
+        h_bf, h_codes, h_sc, y_ps, neg_top = {}, {}, {}, {}, {}
+
+        def project(t):
+            cols = slice(t * P, (t + 1) * P)
+            h_ps = psum_h.tile([P, PACK, P], F32, name="h_ps")
+            for j in range(PACK):
+                for o in range(PASSES):
+                    rhs = x0_g[:, cols] if o == 0 else x1_g[t][:]
+                    nc.tensor.matmul_mx(
+                        out=h_ps[:, j, :],
+                        lhsT=w_codes[o][:, j * P : (j + 1) * P].bitcast(FP8X4),
+                        lhsT_scale=w_sc[o][:, j * P : (j + 1) * P],
+                        rhs=rhs.bitcast(FP8X4),
+                        rhs_scale=xs_g[4 * o : P, cols],
+                        start=(o == 0),
+                        stop=(o == PASSES - 1),
+                    )
+            h_bf[t] = sb("h_bf%d" % t, [P, P, PACK], BF16)
+            nc.scalar.copy(h_bf[t][:], h_ps[:].rearrange("p j t -> p t j"))
+
+        def quant_h(t):
+            if t == 0:
+                h_codes[t] = sb("h_codes0", [P, P], U32)
+            else:
+                h_codes[t] = at("h_codes%d" % t, 23 * kb + 512 * t, [P, P], U32)
+            h_sc[t] = sb("h_sc%d" % t, [P, P], U8)
+            nc.vector.quantize_mx(
+                out=h_codes[t][:].bitcast(FP8X4), scales=h_sc[t][:], in_=h_bf[t][:].rearrange("p t j -> p (t j)")
+            )
+
+        def bank_scores(t):
+            y_ps[t] = psum_y.tile([P, U], F32, name="y_ps")
+            nc.tensor.matmul_mx(
+                out=y_ps[t][:], lhsT=h_codes[t][:].bitcast(FP8X4), lhsT_scale=h_sc[t][:],
+                rhs=e_g[:].bitcast(FP8X4), rhs_scale=es_g[E_ROW:P, :], start=True, stop=True,
+            )
+
+        def row_max(t):
+            neg_top[t] = sb("neg_top%d" % t, [P, 1], F32)
+            nc.vector.tensor_reduce(neg_top[t][:], y_ps[t][:], AX.X, ALU.max, negate=True)
+
+        def finish(t):
+            s_ps = psum_s.tile([P, V], F32, name="s_ps")
+            nc.tensor.matmul_mx(
+                out=s_ps[:], lhsT=h_codes[t][:].bitcast(FP8X4), lhsT_scale=h_sc[t][:],
+                rhs=d_g[:].bitcast(FP8X4), rhs_scale=ds_g[D_ROW:P, :], start=True, stop=True,
+            )
+            ex = sb("ex%d" % t, [P, U], F32)
+            total = sb("total%d" % t, [P, 1], F32)
+            nc.scalar.activation(ex[:], y_ps[t][:], ACT.Exp, bias=neg_top[t][:], accum_out=total[:])
+            num = sb("num%d" % t, [P, V], F32)
+            nc.scalar.activation(num[:], s_ps[:], ACT.Exp, bias=neg_top[t][:])
+            inv = sb("inv%d" % t, [P, 1], F32)
+            nc.vector.reciprocal(inv[:], total[:])
+            res = sb("res%d" % t, [P, V], F32)
+            if t < TILES - 1:
+                nc.gpsimd.tensor_scalar(res[:], num[:], inv[:], 0.0, ALU.mult, ALU.add)
+            else:
+                nc.vector.tensor_scalar(res[:], num[:], inv[:], None, ALU.mult)
+            nc.sync.dma_start(out=out[t * P : (t + 1) * P, :], in_=res[:])
+
+        project(0)
+        nc.vector.tensor_copy(ds_g[:], ds_win[:].indirect(qry_t[:]))
+        quant_h(0)
+        project(1)
+        nc.vector.tensor_copy(e_g[:], ew_win[:].indirect(bank_t[:]))
+        bank_scores(0)
+        quant_h(1)
+        project(2)
+        row_max(0)
+        bank_scores(1)
+        nc.vector.tensor_copy(d_g[:], dw_win[:].indirect(qry_t[:]))
+        quant_h(2)
+        project(3)
+        bank_scores(2)
+        row_max(1)
+        quant_h(3)
+        bank_scores(3)
+        finish(0)
+        row_max(2)
+        finish(1)
+        row_max(3)
+        finish(2)
+        finish(3)

@@ -30,8 +30,8 @@ def tile_picked_yqbn_norm_p_kernel(
     nc = tc.nc
     with ExitStack() as ctx:
         keep = ctx.enter_context(tc.tile_pool(name="keep", bufs=1))
-        psum_h = ctx.enter_context(tc.psum_pool(name="psum_h", bufs=2))
-        psum_y = ctx.enter_context(tc.psum_pool(name="psum_y", bufs=4))
+        psum_h = ctx.enter_context(tc.psum_pool(name="psum_h", bufs=3))
+        psum_y = ctx.enter_context(tc.psum_pool(name="psum_y", bufs=3))
         psum_s = ctx.enter_context(tc.psum_pool(name="psum_s", bufs=2))
 
         def sb(name, shape, dtype):
@@ -45,22 +45,22 @@ def tile_picked_yqbn_norm_p_kernel(
         def at(name, offset, shape, dtype):
             return stage.tile(shape, dtype, name=name, offset=offset, align_bytes=64)
 
-        half = H // 2
         kb = 1024
         es_win = sb("es_win", [P, W], U8)
-        warm = at("warm", 0, [P, 10 * kb // 4], F32)
-        x0_hold = at("x0_hold", 10 * kb, [P, 9 * kb // 4], U32)
-        w0a_hold = at("w0a_hold", 19 * kb, [P, 12 * kb // 4], F32)
-        x0_win = x0_hold[:, 0:T]
-        w0a = w0a_hold[:, 0 : PACK * half].rearrange("p (j i) -> p j i", j=PACK)
+        xs_win = at("xs_win", 27 * kb, [P, T], U8)
+        ds_win = at("ds_win", 25 * kb, [P, G], U8)
+        x0_win = sb("x0_win", [P, T], U32)
+        w0 = sb("w0", [P, PACK, H], F32)
+        warm_out = at("warm_out", kb, [P, 24 * kb // 4], F32)
 
         nc.vector.memset(es_win[:].bitcast(I32), 0)
-        nc.vector.memset(warm[:, 0:8], 0.0)
-        warm_out = sb("warm_out", [P, 8], F32)
-        nc.scalar.activation(warm_out[:], warm[:, 0:8], ACT.Exp)
+        nc.vector.memset(xs_win[:].bitcast(I32), 0)
+        nc.vector.memset(w0[:, 3, 0:8], 0.0)
+        nc.vector.memset(ds_win[:].bitcast(I32), 0)
+        nc.scalar.activation(warm_out[:, 0:8], w0[:, 3, 0:8], ACT.Exp)
 
         def load_w(raw, rows):
-            nc.sync.dma_start(out=raw, in_=rows.rearrange("(p j) i -> p j i", j=PACK))
+            nc.sync.dma_start(out=raw, in_=rows)
 
         def load_words(win, words):
             nc.sync.dma_start(out=win.bitcast(I32), in_=words.rearrange("p n t -> p (n t)").bitcast(I32))
@@ -72,13 +72,13 @@ def tile_picked_yqbn_norm_p_kernel(
                 in_=scales[:, 4 * q : 4 * q + 4, :].bitcast(I32),
             )
 
-        w_bf = [sb("w_bf%d" % o, [P, PACK, P, PACK], BF16) for o in range(PASSES)]
+        w_bf = [at("w_bf%d" % o, (28 + 4 * o) * kb, [P, PACK, P, PACK], BF16) for o in range(PASSES)]
         w_codes = [sb("w_codes%d" % o, [P, H], U32) for o in range(PASSES)]
         w_sc = [sb("w_sc%d" % o, [P, H], U8) for o in range(PASSES)]
 
-        def weave_w(copy, raw, o, c):
-            src = raw.rearrange("p j (m t) -> p m t j", t=PACK)
-            dst = w_bf[o][:, :, c * 64 : (c + 1) * 64, :].rearrange("p t m j -> p m t j")
+        def weave_w(copy, raw, o, m0, m1):
+            src = raw[:, :, PACK * m0 : PACK * m1].rearrange("p j (m t) -> p m t j", t=PACK)
+            dst = w_bf[o][:, :, m0:m1, :].rearrange("p t m j -> p m t j")
             copy(dst, src)
 
         def quant_w(o):
@@ -88,49 +88,40 @@ def tile_picked_yqbn_norm_p_kernel(
 
         xs_g = sb("xs_g", [P, S], U8)
         es_g = sb("es_g", [P, U], U8)
-        ds_g = sb("ds_g", [P, V], U8)
-        x0_g = sb("x0_g", [P, S], U32)
-        x1_g = [sb("x1_g%d" % t, [P, P], U32) for t in range(TILES)]
-        e_g = sb("e_g", [P, U], U32)
         d_g = sb("d_g", [P, V], U32)
+        x0_g = sb("x0_g", [P, S], U32)
 
+        w_rows = w1.rearrange("(o p j) i -> o p j i", o=PASSES, j=PACK)
         nc.sync.dma_start(offs_t[:], offs)
         nc.sync.dma_start(bank_t[:], bank)
+        load_words(x0_win[:], x_words[0])
         nc.sync.dma_start(qry_t[:], qry)
-        load_words(x0_win, x_words[0])
-        load_w(w0a, w1[0:512, 0:half])
+        load_w(w0[:, 0:2, :], w_rows[0][:, 0:2, :])
         for q in range(4):
             load_scales(nc.sync, es_win, E_ROW, e_scales, q)
-
-        w0b = at("w0b", 0, [P, PACK, half], F32)
-        w1a = at("w1a", 4 * kb, [P, PACK, half], F32)
-        xs_win = at("xs_win", 8 * kb, [P, T], U8)
-        load_w(w0b[:], w1[0:512, half:H])
-        load_w(w1a[:], w1[512:1024, 0:half])
-        nc.vector.memset(xs_win[:].bitcast(I32), 0)
         for q in range(4):
-            load_scales(nc.sync, xs_win, 0, x_scales, q)
+            load_scales(nc.sync if q < 2 else nc.gpsimd, xs_win, 0, x_scales, q)
+        for q in range(4):
+            load_scales(nc.gpsimd, ds_win, D_ROW, d_scales, q)
 
-        nc.vector.tensor_copy(x0_g[:], x0_win.indirect(offs_t[:]))
-        w1b = at("w1b", 10 * kb, [P, PACK, half], F32)
-        x1_win = at("x1_win", 14 * kb, [P, T], U32)
-        ds_win = at("ds_win", 18 * kb, [P, G], U8)
-        load_w(w1b[:], w1[512:1024, half:H])
+        load_w(w0[:, 2:4, :], w_rows[0][:, 2:4, :])
+        w1t = at("w1t", kb, [P, PACK, H], F32)
+        x1_win = at("x1_win", 9 * kb, [P, T], U32)
+        ew_win = at("ew_win", 13 * kb, [P, W], U32)
+        dw_win = at("dw_win", 21 * kb, [P, G], U32)
+        load_w(w1t[:], w_rows[1])
         load_words(x1_win[:], x_words[1])
-        nc.vector.memset(ds_win[:].bitcast(I32), 0)
-        for q in range(4):
-            load_scales(nc.sync, ds_win, D_ROW, d_scales, q)
-
-        weave_w(nc.scalar.copy, w0a, 0, 0)
-        ew_win = at("ew_win", 23 * kb, [P, W], U32)
-        dw_win = at("dw_win", 19 * kb, [P, G], U32)
         load_words(ew_win[:], e_words[0])
         load_words(dw_win[:], d_words[0])
 
+        nc.vector.tensor_copy(x0_g[:], x0_win[:].indirect(offs_t[:]))
         nc.vector.tensor_copy(es_g[:], es_win[:].indirect(bank_t[:]))
-        weave_w(nc.vector.tensor_copy, w0b[:], 0, 1)
-        quant_w(0)
         nc.vector.tensor_copy(xs_g[:], xs_win[:].indirect(offs_t[:]))
+        weave_w(nc.scalar.copy, w0, 0, 0, 104)
+        weave_w(nc.vector.tensor_copy, w0, 0, 104, P)
+        ds_g = at("ds_g", 27 * kb, [P, V], U8)
+        nc.vector.tensor_copy(ds_g[:], ds_win[:].indirect(qry_t[:]))
+        quant_w(0)
         warm_ps = psum_y.tile([P, U], F32, name="y_ps")
         for j in range(3):
             nc.tensor.matmul_mx(
@@ -138,9 +129,11 @@ def tile_picked_yqbn_norm_p_kernel(
                 lhsT_scale=w_sc[0][:, j * P : (j + 1) * P],
                 rhs=x0_g[:].bitcast(FP8X4), rhs_scale=xs_g[:], start=True, stop=True,
             )
-        weave_w(nc.scalar.copy, w1a[:], 1, 0)
-        weave_w(nc.vector.tensor_copy, w1b[:], 1, 1)
+        weave_w(nc.scalar.copy, w1t, 1, 0, 56)
+        weave_w(nc.vector.tensor_copy, w1t, 1, 56, P)
         quant_w(1)
+        x1_g = [sb("x1_g0", [P, P], U32)]
+        x1_g.extend(at("x1_g%d" % t, 32 * kb + 512 * t, [P, P], U32) for t in range(1, TILES))
         for t in range(TILES):
             nc.vector.tensor_copy(x1_g[t][:], x1_win[:].indirect(offs_t[:, 8 * t : 8 * t + 8]))
 
@@ -165,10 +158,7 @@ def tile_picked_yqbn_norm_p_kernel(
             nc.scalar.copy(h_bf[t][:], h_ps[:].rearrange("p j t -> p t j"))
 
         def quant_h(t):
-            if t == 0:
-                h_codes[t] = sb("h_codes0", [P, P], U32)
-            else:
-                h_codes[t] = at("h_codes%d" % t, 23 * kb + 512 * t, [P, P], U32)
+            h_codes[t] = at("h_codes%d" % t, 13 * kb if t % 2 else 0, [P, P], U32)
             h_sc[t] = sb("h_sc%d" % t, [P, P], U8)
             nc.vector.quantize_mx(
                 out=h_codes[t][:].bitcast(FP8X4), scales=h_sc[t][:], in_=h_bf[t][:].rearrange("p t j -> p (t j)")
@@ -206,25 +196,25 @@ def tile_picked_yqbn_norm_p_kernel(
             nc.sync.dma_start(out=out[t * P : (t + 1) * P, :], in_=res[:])
 
         project(0)
-        nc.vector.tensor_copy(ds_g[:], ds_win[:].indirect(qry_t[:]))
         quant_h(0)
         project(1)
+        e_g = at("e_g", 25 * kb, [P, U], U32)
         nc.vector.tensor_copy(e_g[:], ew_win[:].indirect(bank_t[:]))
         bank_scores(0)
         quant_h(1)
         project(2)
+        project(3)
         row_max(0)
         bank_scores(1)
         nc.vector.tensor_copy(d_g[:], dw_win[:].indirect(qry_t[:]))
-        quant_h(2)
-        project(3)
-        bank_scores(2)
+        finish(0)
         row_max(1)
+        quant_h(2)
+        bank_scores(2)
+        finish(1)
         quant_h(3)
         bank_scores(3)
-        finish(0)
         row_max(2)
-        finish(1)
-        row_max(3)
         finish(2)
+        row_max(3)
         finish(3)

@@ -46,17 +46,15 @@ def tile_picked_yqbn_norm_p_kernel(
             return stage.tile(shape, dtype, name=name, offset=offset, align_bytes=64)
 
         kb = 1024
-        es_win = sb("es_win", [P, W], U8)
-        xs_win = at("xs_win", 27 * kb, [P, T], U8)
-        ds_win = at("ds_win", 25 * kb, [P, G], U8)
-        x0_win = sb("x0_win", [P, T], U32)
         w0 = sb("w0", [P, PACK, H], F32)
-        warm_out = at("warm_out", kb, [P, 24 * kb // 4], F32)
+        x0_hold = at("x0_hold", 4 * kb, [P, 9 * kb // 4], U32)
+        es_hold = at("es_hold", 13 * kb, [P, 14 * kb], U8)
+        warm_out = at("warm_out", 36 * kb, [P, 7 * kb // 4], F32)
+        x0_win = x0_hold[:, 0:T]
+        es_win = es_hold[:, 0:W]
 
-        nc.vector.memset(es_win[:].bitcast(I32), 0)
-        nc.vector.memset(xs_win[:].bitcast(I32), 0)
+        nc.vector.memset(es_win.bitcast(I32), 0)
         nc.vector.memset(w0[:, 3, 0:8], 0.0)
-        nc.vector.memset(ds_win[:].bitcast(I32), 0)
         nc.scalar.activation(warm_out[:, 0:8], w0[:, 3, 0:8], ACT.Exp)
 
         def load_w(raw, rows):
@@ -76,8 +74,8 @@ def tile_picked_yqbn_norm_p_kernel(
         w_codes = [sb("w_codes%d" % o, [P, H], U32) for o in range(PASSES)]
         w_sc = [sb("w_sc%d" % o, [P, H], U8) for o in range(PASSES)]
 
-        def weave_w(copy, raw, o, m0, m1):
-            src = raw[:, :, PACK * m0 : PACK * m1].rearrange("p j (m t) -> p m t j", t=PACK)
+        def weave_w(copy, raw, o, m0, m1, first=0):
+            src = raw[:, :, PACK * (m0 - first) : PACK * (m1 - first)].rearrange("p j (m t) -> p m t j", t=PACK)
             dst = w_bf[o][:, :, m0:m1, :].rearrange("p t m j -> p m t j")
             copy(dst, src)
 
@@ -89,48 +87,56 @@ def tile_picked_yqbn_norm_p_kernel(
         xs_g = sb("xs_g", [P, S], U8)
         es_g = sb("es_g", [P, U], U8)
         d_g = sb("d_g", [P, V], U32)
-        x0_g = sb("x0_g", [P, S], U32)
+        e_g = sb("e_g", [P, U], U32)
 
         w_rows = w1.rearrange("(o p j) i -> o p j i", o=PASSES, j=PACK)
         nc.sync.dma_start(offs_t[:], offs)
         nc.sync.dma_start(bank_t[:], bank)
-        load_words(x0_win[:], x_words[0])
+        load_words(x0_win, x_words[0])
         nc.sync.dma_start(qry_t[:], qry)
         load_w(w0[:, 0:2, :], w_rows[0][:, 0:2, :])
         for q in range(4):
             load_scales(nc.sync, es_win, E_ROW, e_scales, q)
-        for q in range(4):
-            load_scales(nc.sync if q < 2 else nc.gpsimd, xs_win, 0, x_scales, q)
-        for q in range(4):
-            load_scales(nc.gpsimd, ds_win, D_ROW, d_scales, q)
 
         load_w(w0[:, 2:4, :], w_rows[0][:, 2:4, :])
-        w1t = at("w1t", kb, [P, PACK, H], F32)
-        x1_win = at("x1_win", 9 * kb, [P, T], U32)
-        ew_win = at("ew_win", 13 * kb, [P, W], U32)
-        dw_win = at("dw_win", 21 * kb, [P, G], U32)
-        load_w(w1t[:], w_rows[1])
+        w1a = at("w1a", 39 * kb, [P, PACK, H // 2], F32)
+        load_w(w1a[:], w_rows[1][:, :, 0 : H // 2])
+        xs_win = at("xs_win", 36 * kb, [P, T], U8)
+        nc.vector.memset(xs_win[:].bitcast(I32), 0)
+        for q in range(4):
+            load_scales(nc.sync, xs_win, 0, x_scales, q)
+
+        x0_g = at("x0_g", 37 * kb, [P, S], U32)
+        nc.vector.tensor_copy(x0_g[:], x0_win.indirect(offs_t[:]))
+        w1b = at("w1b", 4 * kb, [P, PACK, H // 2], F32)
+        x1_win = at("x1_win", 8 * kb, [P, T], U32)
+        ds_win = at("ds_win", 12 * kb, [P, G], U8)
+        load_w(w1b[:], w_rows[1][:, :, H // 2 : H])
         load_words(x1_win[:], x_words[1])
+        nc.vector.memset(ds_win[:].bitcast(I32), 0)
+        for q in range(4):
+            load_scales(nc.sync, ds_win, D_ROW, d_scales, q)
+
+        nc.vector.tensor_copy(es_g[:], es_win.indirect(bank_t[:]))
+        ew_win = at("ew_win", 15 * kb, [P, W], U32)
+        dw_win = at("dw_win", 23 * kb, [P, G], U32)
         load_words(ew_win[:], e_words[0])
         load_words(dw_win[:], d_words[0])
 
-        nc.vector.tensor_copy(x0_g[:], x0_win[:].indirect(offs_t[:]))
-        nc.vector.tensor_copy(es_g[:], es_win[:].indirect(bank_t[:]))
-        nc.vector.tensor_copy(xs_g[:], xs_win[:].indirect(offs_t[:]))
-        weave_w(nc.scalar.copy, w0, 0, 0, 104)
-        weave_w(nc.vector.tensor_copy, w0, 0, 104, P)
-        ds_g = at("ds_g", 27 * kb, [P, V], U8)
-        nc.vector.tensor_copy(ds_g[:], ds_win[:].indirect(qry_t[:]))
+        weave_w(nc.scalar.copy, w0, 0, 0, 56)
+        weave_w(nc.vector.tensor_copy, w0, 0, 56, P)
         quant_w(0)
+        nc.vector.tensor_copy(xs_g[:], xs_win[:].indirect(offs_t[:]))
         warm_ps = psum_y.tile([P, U], F32, name="y_ps")
-        for j in range(3):
+        for j in range(2):
             nc.tensor.matmul_mx(
                 out=warm_ps[:], lhsT=w_codes[0][:, j * P : (j + 1) * P].bitcast(FP8X4),
                 lhsT_scale=w_sc[0][:, j * P : (j + 1) * P],
                 rhs=x0_g[:].bitcast(FP8X4), rhs_scale=xs_g[:], start=True, stop=True,
             )
-        weave_w(nc.scalar.copy, w1t, 1, 0, 56)
-        weave_w(nc.vector.tensor_copy, w1t, 1, 56, P)
+        weave_w(nc.scalar.copy, w1a, 1, 0, 64)
+        weave_w(nc.scalar.copy, w1b, 1, 64, 100, 64)
+        weave_w(nc.vector.tensor_copy, w1b, 1, 100, P, 64)
         quant_w(1)
         x1_g = [sb("x1_g0", [P, P], U32)]
         x1_g.extend(at("x1_g%d" % t, 32 * kb + 512 * t, [P, P], U32) for t in range(1, TILES))
@@ -158,7 +164,7 @@ def tile_picked_yqbn_norm_p_kernel(
             nc.scalar.copy(h_bf[t][:], h_ps[:].rearrange("p j t -> p t j"))
 
         def quant_h(t):
-            h_codes[t] = at("h_codes%d" % t, 13 * kb if t % 2 else 0, [P, P], U32)
+            h_codes[t] = at("h_codes%d" % t, 15 * kb + 512 * (t % 3), [P, P], U32)
             h_sc[t] = sb("h_sc%d" % t, [P, P], U8)
             nc.vector.quantize_mx(
                 out=h_codes[t][:].bitcast(FP8X4), scales=h_sc[t][:], in_=h_bf[t][:].rearrange("p t j -> p (t j)")
@@ -195,26 +201,25 @@ def tile_picked_yqbn_norm_p_kernel(
                 nc.vector.tensor_scalar(res[:], num[:], inv[:], None, ALU.mult)
             nc.sync.dma_start(out=out[t * P : (t + 1) * P, :], in_=res[:])
 
-        project(0)
-        quant_h(0)
-        project(1)
-        e_g = at("e_g", 25 * kb, [P, U], U32)
+        for t in range(TILES):
+            project(t)
         nc.vector.tensor_copy(e_g[:], ew_win[:].indirect(bank_t[:]))
+        quant_h(0)
         bank_scores(0)
         quant_h(1)
-        project(2)
-        project(3)
-        row_max(0)
         bank_scores(1)
-        nc.vector.tensor_copy(d_g[:], dw_win[:].indirect(qry_t[:]))
-        finish(0)
-        row_max(1)
+        ds_g = at("ds_g", 17 * kb, [P, V], U8)
+        nc.vector.tensor_copy(ds_g[:], ds_win[:].indirect(qry_t[:]))
         quant_h(2)
         bank_scores(2)
-        finish(1)
+        row_max(0)
+        nc.vector.tensor_copy(d_g[:], dw_win[:].indirect(qry_t[:]))
+        row_max(1)
+        finish(0)
         quant_h(3)
         bank_scores(3)
+        finish(1)
         row_max(2)
-        finish(2)
         row_max(3)
+        finish(2)
         finish(3)

@@ -30,9 +30,8 @@ def tile_picked_yqbn_norm_p_kernel(
     nc = tc.nc
     with ExitStack() as ctx:
         keep = ctx.enter_context(tc.tile_pool(name="keep", bufs=1))
-        psum_h = ctx.enter_context(tc.psum_pool(name="psum_h", bufs=3))
-        psum_y = ctx.enter_context(tc.psum_pool(name="psum_y", bufs=3))
-        psum_s = ctx.enter_context(tc.psum_pool(name="psum_s", bufs=2))
+        psum_h = ctx.enter_context(tc.psum_pool(name="psum_h", bufs=4))
+        psum_y = ctx.enter_context(tc.psum_pool(name="psum_y", bufs=4))
 
         def sb(name, shape, dtype):
             return keep.tile(shape, dtype, name=name, align_bytes=64)
@@ -47,13 +46,13 @@ def tile_picked_yqbn_norm_p_kernel(
 
         kb = 1024
         w0 = sb("w0", [P, PACK, H], F32)
-        x0_hold = at("x0_hold", 4 * kb, [P, 9 * kb // 4], U32)
-        es_hold = at("es_hold", 13 * kb, [P, 14 * kb], U8)
-        warm_out = at("warm_out", 36 * kb, [P, 7 * kb // 4], F32)
+        x0_hold = at("x0_hold", 4 * kb, [P, 10 * kb // 4], U32)
+        xs_hold = at("xs_hold", 14 * kb, [P, 14 * kb], U8)
+        warm_out = at("warm_out", 36 * kb, [P, 8 * kb // 4], F32)
         x0_win = x0_hold[:, 0:T]
-        es_win = es_hold[:, 0:W]
+        xs_win = xs_hold[:, 0:T]
 
-        nc.vector.memset(es_win.bitcast(I32), 0)
+        nc.vector.memset(xs_win.bitcast(I32), 0)
         nc.vector.memset(w0[:, 3, 0:8], 0.0)
         nc.scalar.activation(warm_out[:, 0:8], w0[:, 3, 0:8], ACT.Exp)
 
@@ -96,52 +95,57 @@ def tile_picked_yqbn_norm_p_kernel(
         nc.sync.dma_start(qry_t[:], qry)
         load_w(w0[:, 0:2, :], w_rows[0][:, 0:2, :])
         for q in range(4):
-            load_scales(nc.sync, es_win, E_ROW, e_scales, q)
-
-        load_w(w0[:, 2:4, :], w_rows[0][:, 2:4, :])
-        w1a = at("w1a", 39 * kb, [P, PACK, H // 2], F32)
-        load_w(w1a[:], w_rows[1][:, :, 0 : H // 2])
-        xs_win = at("xs_win", 36 * kb, [P, T], U8)
-        nc.vector.memset(xs_win[:].bitcast(I32), 0)
-        for q in range(4):
             load_scales(nc.sync, xs_win, 0, x_scales, q)
 
-        x0_g = at("x0_g", 37 * kb, [P, S], U32)
+        load_w(w0[:, 2:4, :], w_rows[0][:, 2:4, :])
+        w1a = at("w1a", 40 * kb, [P, PACK, H // 2], F32)
+        load_w(w1a[:], w_rows[1][:, :, 0 : H // 2])
+        es_win = at("es_win", 36 * kb, [P, W], U8)
+        nc.vector.memset(es_win[:].bitcast(I32), 0)
+        for q in range(4):
+            load_scales(nc.sync, es_win, E_ROW, e_scales, q)
+
+        x0_g = at("x0_g", 38 * kb, [P, S], U32)
         nc.vector.tensor_copy(x0_g[:], x0_win.indirect(offs_t[:]))
         w1b = at("w1b", 4 * kb, [P, PACK, H // 2], F32)
         x1_win = at("x1_win", 8 * kb, [P, T], U32)
         ds_win = at("ds_win", 12 * kb, [P, G], U8)
         load_w(w1b[:], w_rows[1][:, :, H // 2 : H])
         load_words(x1_win[:], x_words[1])
-        nc.vector.memset(ds_win[:].bitcast(I32), 0)
+        nc.gpsimd.memset(ds_win[:].bitcast(I32), 0)
         for q in range(4):
             load_scales(nc.sync, ds_win, D_ROW, d_scales, q)
 
-        nc.vector.tensor_copy(es_g[:], es_win.indirect(bank_t[:]))
-        ew_win = at("ew_win", 15 * kb, [P, W], U32)
-        dw_win = at("dw_win", 23 * kb, [P, G], U32)
+        nc.vector.tensor_copy(xs_g[:], xs_win.indirect(offs_t[:]))
+        ew_win = at("ew_win", 16 * kb, [P, W], U32)
+        dw_win = at("dw_win", 24 * kb, [P, G], U32)
         load_words(ew_win[:], e_words[0])
         load_words(dw_win[:], d_words[0])
 
         weave_w(nc.scalar.copy, w0, 0, 0, 56)
         weave_w(nc.vector.tensor_copy, w0, 0, 56, P)
+        nc.vector.tensor_copy(es_g[:], es_win[:].indirect(bank_t[:]))
         quant_w(0)
-        nc.vector.tensor_copy(xs_g[:], xs_win[:].indirect(offs_t[:]))
         warm_ps = psum_y.tile([P, U], F32, name="y_ps")
-        for j in range(2):
+        for j in range(3):
             nc.tensor.matmul_mx(
                 out=warm_ps[:], lhsT=w_codes[0][:, j * P : (j + 1) * P].bitcast(FP8X4),
                 lhsT_scale=w_sc[0][:, j * P : (j + 1) * P],
                 rhs=x0_g[:].bitcast(FP8X4), rhs_scale=xs_g[:], start=True, stop=True,
             )
         weave_w(nc.scalar.copy, w1a, 1, 0, 64)
-        weave_w(nc.scalar.copy, w1b, 1, 64, 100, 64)
-        weave_w(nc.vector.tensor_copy, w1b, 1, 100, P, 64)
+        weave_w(nc.scalar.copy, w1b, 1, 64, P, 64)
         quant_w(1)
-        x1_g = [sb("x1_g0", [P, P], U32)]
-        x1_g.extend(at("x1_g%d" % t, 32 * kb + 512 * t, [P, P], U32) for t in range(1, TILES))
-        for t in range(TILES):
-            nc.vector.tensor_copy(x1_g[t][:], x1_win[:].indirect(offs_t[:, 8 * t : 8 * t + 8]))
+        x1_first = sb("x1_first", [P, P], U32)
+        x1_rest = at("x1_rest", 4 * kb, [P, S - P], U32)
+        nc.vector.tensor_copy(x1_first[:], x1_win[:].indirect(offs_t[:, 0:8]))
+        nc.vector.tensor_copy(x1_rest[:], x1_win[:].indirect(offs_t[:, 8:32]))
+        x1_g = [x1_first[:]] + [x1_rest[:, (t - 1) * P : t * P] for t in range(1, TILES)]
+        ds_g = at("ds_g", 6 * kb, [P, V], U8)
+        nc.vector.tensor_copy(ds_g[:], ds_win[:].indirect(qry_t[:]))
+
+        minus_one = sb("minus_one", [P, 1], F32)
+        nc.gpsimd.memset(minus_one[:], -1.0)
 
         h_bf, h_codes, h_sc, y_ps, neg_top = {}, {}, {}, {}, {}
 
@@ -150,7 +154,7 @@ def tile_picked_yqbn_norm_p_kernel(
             h_ps = psum_h.tile([P, PACK, P], F32, name="h_ps")
             for j in range(PACK):
                 for o in range(PASSES):
-                    rhs = x0_g[:, cols] if o == 0 else x1_g[t][:]
+                    rhs = x0_g[:, cols] if o == 0 else x1_g[t]
                     nc.tensor.matmul_mx(
                         out=h_ps[:, j, :],
                         lhsT=w_codes[o][:, j * P : (j + 1) * P].bitcast(FP8X4),
@@ -164,7 +168,10 @@ def tile_picked_yqbn_norm_p_kernel(
             nc.scalar.copy(h_bf[t][:], h_ps[:].rearrange("p j t -> p t j"))
 
         def quant_h(t):
-            h_codes[t] = at("h_codes%d" % t, 15 * kb + 512 * (t % 3), [P, P], U32)
+            if t == 0:
+                h_codes[t] = at("h_codes0", 16 * kb, [P, P], U32)
+            else:
+                h_codes[t] = at("h_codes%d" % t, 16 * kb + 512 * t, [P, P], U32)
             h_sc[t] = sb("h_sc%d" % t, [P, P], U8)
             nc.vector.quantize_mx(
                 out=h_codes[t][:].bitcast(FP8X4), scales=h_sc[t][:], in_=h_bf[t][:].rearrange("p t j -> p (t j)")
@@ -182,7 +189,7 @@ def tile_picked_yqbn_norm_p_kernel(
             nc.vector.tensor_reduce(neg_top[t][:], y_ps[t][:], AX.X, ALU.max, negate=True)
 
         def finish(t):
-            s_ps = psum_s.tile([P, V], F32, name="s_ps")
+            s_ps = psum_h.tile([P, V], F32, name="h_ps")
             nc.tensor.matmul_mx(
                 out=s_ps[:], lhsT=h_codes[t][:].bitcast(FP8X4), lhsT_scale=h_sc[t][:],
                 rhs=d_g[:].bitcast(FP8X4), rhs_scale=ds_g[D_ROW:P, :], start=True, stop=True,
@@ -193,11 +200,12 @@ def tile_picked_yqbn_norm_p_kernel(
             num = sb("num%d" % t, [P, V], F32)
             nc.scalar.activation(num[:], s_ps[:], ACT.Exp, bias=neg_top[t][:])
             inv = sb("inv%d" % t, [P, 1], F32)
-            nc.vector.reciprocal(inv[:], total[:])
             res = sb("res%d" % t, [P, V], F32)
-            if t < TILES - 1:
+            if t < 2:
+                nc.gpsimd.tensor_tensor(inv[:], total[:], minus_one[:], ALU.pow)
                 nc.gpsimd.tensor_scalar(res[:], num[:], inv[:], 0.0, ALU.mult, ALU.add)
             else:
+                nc.vector.reciprocal(inv[:], total[:])
                 nc.vector.tensor_scalar(res[:], num[:], inv[:], None, ALU.mult)
             nc.sync.dma_start(out=out[t * P : (t + 1) * P, :], in_=res[:])
 
@@ -208,8 +216,6 @@ def tile_picked_yqbn_norm_p_kernel(
         bank_scores(0)
         quant_h(1)
         bank_scores(1)
-        ds_g = at("ds_g", 17 * kb, [P, V], U8)
-        nc.vector.tensor_copy(ds_g[:], ds_win[:].indirect(qry_t[:]))
         quant_h(2)
         bank_scores(2)
         row_max(0)

@@ -22,6 +22,7 @@ PASSES = K // (P * PACK)
 TILES = S // P
 E_ROW = 8
 D_ROW = 12
+QUADS = (0, 2, 1, 3)
 
 
 def tile_picked_yqbn_norm_p_kernel(
@@ -74,14 +75,19 @@ def tile_picked_yqbn_norm_p_kernel(
         w_sc = [sb("w_sc%d" % o, [P, H], U8) for o in range(PASSES)]
 
         def weave_w(copy, raw, o, m0, m1, first=0):
-            src = raw[:, :, PACK * (m0 - first) : PACK * (m1 - first)].rearrange("p j (m t) -> p m t j", t=PACK)
-            dst = w_bf[o][:, :, m0:m1, :].rearrange("p t m j -> p m t j")
+            src = raw[:, :, PACK * (m0 - first) : PACK * (m1 - first)].rearrange("p j (m t) -> p m j t", t=PACK)
+            dst = w_bf[o][:, :, m0:m1, :].rearrange("p t m j -> p m j t")
             copy(dst, src)
 
         def quant_w(o):
             nc.vector.quantize_mx(
                 out=w_codes[o][:].bitcast(FP8X4), scales=w_sc[o][:], in_=w_bf[o][:].rearrange("p t m j -> p (t m j)")
             )
+
+        ds_win = sb("ds_win", [P, G], U8)
+        nc.gpsimd.memset(ds_win[:].bitcast(I32), 0)
+        for q in QUADS:
+            load_scales(nc.gpsimd, ds_win, D_ROW, d_scales, q)
 
         xs_g = sb("xs_g", [P, S], U8)
         es_g = sb("es_g", [P, U], U8)
@@ -94,7 +100,7 @@ def tile_picked_yqbn_norm_p_kernel(
         load_words(x0_win, x_words[0])
         nc.sync.dma_start(qry_t[:], qry)
         load_w(w0[:, 0:2, :], w_rows[0][:, 0:2, :])
-        for q in range(4):
+        for q in QUADS:
             load_scales(nc.sync, xs_win, 0, x_scales, q)
 
         load_w(w0[:, 2:4, :], w_rows[0][:, 2:4, :])
@@ -102,19 +108,15 @@ def tile_picked_yqbn_norm_p_kernel(
         load_w(w1a[:], w_rows[1][:, :, 0 : H // 2])
         es_win = at("es_win", 36 * kb, [P, W], U8)
         nc.vector.memset(es_win[:].bitcast(I32), 0)
-        for q in range(4):
+        for q in QUADS:
             load_scales(nc.sync, es_win, E_ROW, e_scales, q)
 
         x0_g = at("x0_g", 38 * kb, [P, S], U32)
         nc.vector.tensor_copy(x0_g[:], x0_win.indirect(offs_t[:]))
         w1b = at("w1b", 4 * kb, [P, PACK, H // 2], F32)
         x1_win = at("x1_win", 8 * kb, [P, T], U32)
-        ds_win = at("ds_win", 12 * kb, [P, G], U8)
         load_w(w1b[:], w_rows[1][:, :, H // 2 : H])
         load_words(x1_win[:], x_words[1])
-        nc.gpsimd.memset(ds_win[:].bitcast(I32), 0)
-        for q in range(4):
-            load_scales(nc.sync, ds_win, D_ROW, d_scales, q)
 
         nc.vector.tensor_copy(xs_g[:], xs_win.indirect(offs_t[:]))
         ew_win = at("ew_win", 16 * kb, [P, W], U32)
@@ -134,7 +136,8 @@ def tile_picked_yqbn_norm_p_kernel(
                 rhs=x0_g[:].bitcast(FP8X4), rhs_scale=xs_g[:], start=True, stop=True,
             )
         weave_w(nc.scalar.copy, w1a, 1, 0, 64)
-        weave_w(nc.scalar.copy, w1b, 1, 64, P, 64)
+        weave_w(nc.scalar.copy, w1b, 1, 64, 104, 64)
+        weave_w(nc.vector.tensor_copy, w1b, 1, 104, P, 64)
         quant_w(1)
         x1_first = sb("x1_first", [P, P], U32)
         x1_rest = at("x1_rest", 4 * kb, [P, S - P], U32)
@@ -143,9 +146,6 @@ def tile_picked_yqbn_norm_p_kernel(
         x1_g = [x1_first[:]] + [x1_rest[:, (t - 1) * P : t * P] for t in range(1, TILES)]
         ds_g = at("ds_g", 6 * kb, [P, V], U8)
         nc.vector.tensor_copy(ds_g[:], ds_win[:].indirect(qry_t[:]))
-
-        minus_one = sb("minus_one", [P, 1], F32)
-        nc.gpsimd.memset(minus_one[:], -1.0)
 
         h_bf, h_codes, h_sc, y_ps, neg_top = {}, {}, {}, {}, {}
 
@@ -188,26 +188,27 @@ def tile_picked_yqbn_norm_p_kernel(
             neg_top[t] = sb("neg_top%d" % t, [P, 1], F32)
             nc.vector.tensor_reduce(neg_top[t][:], y_ps[t][:], AX.X, ALU.max, negate=True)
 
-        def finish(t):
+        total = sb("total", [P, TILES], F32)
+        inv = sb("inv", [P, TILES], F32)
+        num = {}
+
+        def exps(t):
             s_ps = psum_h.tile([P, V], F32, name="h_ps")
             nc.tensor.matmul_mx(
                 out=s_ps[:], lhsT=h_codes[t][:].bitcast(FP8X4), lhsT_scale=h_sc[t][:],
                 rhs=d_g[:].bitcast(FP8X4), rhs_scale=ds_g[D_ROW:P, :], start=True, stop=True,
             )
             ex = sb("ex%d" % t, [P, U], F32)
-            total = sb("total%d" % t, [P, 1], F32)
-            nc.scalar.activation(ex[:], y_ps[t][:], ACT.Exp, bias=neg_top[t][:], accum_out=total[:])
-            num = sb("num%d" % t, [P, V], F32)
-            nc.scalar.activation(num[:], s_ps[:], ACT.Exp, bias=neg_top[t][:])
-            inv = sb("inv%d" % t, [P, 1], F32)
-            res = sb("res%d" % t, [P, V], F32)
-            if t < 2:
-                nc.gpsimd.tensor_tensor(inv[:], total[:], minus_one[:], ALU.pow)
-                nc.gpsimd.tensor_scalar(res[:], num[:], inv[:], 0.0, ALU.mult, ALU.add)
-            else:
-                nc.vector.reciprocal(inv[:], total[:])
-                nc.vector.tensor_scalar(res[:], num[:], inv[:], None, ALU.mult)
-            nc.sync.dma_start(out=out[t * P : (t + 1) * P, :], in_=res[:])
+            nc.scalar.activation(ex[:], y_ps[t][:], ACT.Exp, bias=neg_top[t][:], accum_out=total[:, t : t + 1])
+            num[t] = sb("num%d" % t, [P, V], F32)
+            nc.scalar.activation(num[t][:], s_ps[:], ACT.Exp, bias=neg_top[t][:])
+
+        def finish(first, last):
+            nc.vector.reciprocal(inv[:, first:last], total[:, first:last])
+            for t in range(first, last):
+                res = sb("res%d" % t, [P, V], F32)
+                nc.vector.tensor_scalar(res[:], num[t][:], inv[:, t : t + 1], None, ALU.mult)
+                nc.sync.dma_start(out=out[t * P : (t + 1) * P, :], in_=res[:])
 
         for t in range(TILES):
             project(t)
@@ -221,11 +222,14 @@ def tile_picked_yqbn_norm_p_kernel(
         row_max(0)
         nc.vector.tensor_copy(d_g[:], dw_win[:].indirect(qry_t[:]))
         row_max(1)
-        finish(0)
+        exps(0)
         quant_h(3)
         bank_scores(3)
-        finish(1)
+        exps(1)
         row_max(2)
         row_max(3)
-        finish(2)
-        finish(3)
+        exps(2)
+        exps(3)
+        finish(0, 2)
+        finish(2, 3)
+        finish(3, 4)

@@ -48,12 +48,12 @@ def tile_picked_yqbn_norm_p_kernel(
         kb = 1024
         w0 = sb("w0", [P, PACK, H], F32)
         x0_hold = at("x0_hold", 4 * kb, [P, 10 * kb // 4], U32)
-        xs_hold = at("xs_hold", 14 * kb, [P, 14 * kb], U8)
+        es_hold = at("es_hold", 14 * kb, [P, 14 * kb], U8)
         warm_out = at("warm_out", 36 * kb, [P, 8 * kb // 4], F32)
         x0_win = x0_hold[:, 0:T]
-        xs_win = xs_hold[:, 0:T]
+        es_win = es_hold[:, 0:W]
 
-        nc.vector.memset(xs_win.bitcast(I32), 0)
+        nc.vector.memset(es_win.bitcast(I32), 0)
         nc.vector.memset(w0[:, 3, 0:8], 0.0)
         nc.scalar.activation(warm_out[:, 0:8], w0[:, 3, 0:8], ACT.Exp)
 
@@ -84,11 +84,6 @@ def tile_picked_yqbn_norm_p_kernel(
                 out=w_codes[o][:].bitcast(FP8X4), scales=w_sc[o][:], in_=w_bf[o][:].rearrange("p t m j -> p (t m j)")
             )
 
-        ds_win = sb("ds_win", [P, G], U8)
-        nc.gpsimd.memset(ds_win[:].bitcast(I32), 0)
-        for q in QUADS:
-            load_scales(nc.gpsimd, ds_win, D_ROW, d_scales, q)
-
         xs_g = sb("xs_g", [P, S], U8)
         es_g = sb("es_g", [P, U], U8)
         d_g = sb("d_g", [P, V], U32)
@@ -101,15 +96,15 @@ def tile_picked_yqbn_norm_p_kernel(
         nc.sync.dma_start(qry_t[:], qry)
         load_w(w0[:, 0:2, :], w_rows[0][:, 0:2, :])
         for q in QUADS:
-            load_scales(nc.sync, xs_win, 0, x_scales, q)
+            load_scales(nc.sync, es_win, E_ROW, e_scales, q)
 
         load_w(w0[:, 2:4, :], w_rows[0][:, 2:4, :])
         w1a = at("w1a", 40 * kb, [P, PACK, H // 2], F32)
         load_w(w1a[:], w_rows[1][:, :, 0 : H // 2])
-        es_win = at("es_win", 36 * kb, [P, W], U8)
-        nc.vector.memset(es_win[:].bitcast(I32), 0)
+        xs_win = at("xs_win", 36 * kb, [P, T], U8)
+        nc.vector.memset(xs_win[:].bitcast(I32), 0)
         for q in QUADS:
-            load_scales(nc.sync, es_win, E_ROW, e_scales, q)
+            load_scales(nc.sync, xs_win, 0, x_scales, q)
 
         x0_g = at("x0_g", 38 * kb, [P, S], U32)
         nc.vector.tensor_copy(x0_g[:], x0_win.indirect(offs_t[:]))
@@ -117,8 +112,12 @@ def tile_picked_yqbn_norm_p_kernel(
         x1_win = at("x1_win", 8 * kb, [P, T], U32)
         load_w(w1b[:], w_rows[1][:, :, H // 2 : H])
         load_words(x1_win[:], x_words[1])
+        ds_win = at("ds_win", 12 * kb, [P, G], U8)
+        nc.gpsimd.memset(ds_win[:].bitcast(I32), 0)
+        for q in QUADS:
+            load_scales(nc.sync, ds_win, D_ROW, d_scales, q)
 
-        nc.vector.tensor_copy(xs_g[:], xs_win.indirect(offs_t[:]))
+        nc.vector.tensor_copy(es_g[:], es_win.indirect(bank_t[:]))
         ew_win = at("ew_win", 16 * kb, [P, W], U32)
         dw_win = at("dw_win", 24 * kb, [P, G], U32)
         load_words(ew_win[:], e_words[0])
@@ -126,18 +125,17 @@ def tile_picked_yqbn_norm_p_kernel(
 
         weave_w(nc.scalar.copy, w0, 0, 0, 56)
         weave_w(nc.vector.tensor_copy, w0, 0, 56, P)
-        nc.vector.tensor_copy(es_g[:], es_win[:].indirect(bank_t[:]))
         quant_w(0)
+        nc.vector.tensor_copy(xs_g[:], xs_win[:].indirect(offs_t[:]))
         warm_ps = psum_y.tile([P, U], F32, name="y_ps")
         for j in range(3):
             nc.tensor.matmul_mx(
                 out=warm_ps[:], lhsT=w_codes[0][:, j * P : (j + 1) * P].bitcast(FP8X4),
                 lhsT_scale=w_sc[0][:, j * P : (j + 1) * P],
-                rhs=x0_g[:].bitcast(FP8X4), rhs_scale=xs_g[:], start=True, stop=True,
+                rhs=x0_g[:].bitcast(FP8X4), rhs_scale=es_g[E_ROW:P, :], start=True, stop=True,
             )
         weave_w(nc.scalar.copy, w1a, 1, 0, 64)
-        weave_w(nc.scalar.copy, w1b, 1, 64, 104, 64)
-        weave_w(nc.vector.tensor_copy, w1b, 1, 104, P, 64)
+        weave_w(nc.scalar.copy, w1b, 1, 64, P, 64)
         quant_w(1)
         x1_first = sb("x1_first", [P, P], U32)
         x1_rest = at("x1_rest", 4 * kb, [P, S - P], U32)
@@ -146,6 +144,9 @@ def tile_picked_yqbn_norm_p_kernel(
         x1_g = [x1_first[:]] + [x1_rest[:, (t - 1) * P : t * P] for t in range(1, TILES)]
         ds_g = at("ds_g", 6 * kb, [P, V], U8)
         nc.vector.tensor_copy(ds_g[:], ds_win[:].indirect(qry_t[:]))
+
+        minus_one = sb("minus_one", [P, 1], F32)
+        nc.gpsimd.memset(minus_one[:], -1.0)
 
         h_bf, h_codes, h_sc, y_ps, neg_top = {}, {}, {}, {}, {}
 
@@ -188,27 +189,26 @@ def tile_picked_yqbn_norm_p_kernel(
             neg_top[t] = sb("neg_top%d" % t, [P, 1], F32)
             nc.vector.tensor_reduce(neg_top[t][:], y_ps[t][:], AX.X, ALU.max, negate=True)
 
-        total = sb("total", [P, TILES], F32)
-        inv = sb("inv", [P, TILES], F32)
-        num = {}
-
-        def exps(t):
+        def finish(t):
             s_ps = psum_h.tile([P, V], F32, name="h_ps")
             nc.tensor.matmul_mx(
                 out=s_ps[:], lhsT=h_codes[t][:].bitcast(FP8X4), lhsT_scale=h_sc[t][:],
                 rhs=d_g[:].bitcast(FP8X4), rhs_scale=ds_g[D_ROW:P, :], start=True, stop=True,
             )
             ex = sb("ex%d" % t, [P, U], F32)
-            nc.scalar.activation(ex[:], y_ps[t][:], ACT.Exp, bias=neg_top[t][:], accum_out=total[:, t : t + 1])
-            num[t] = sb("num%d" % t, [P, V], F32)
-            nc.scalar.activation(num[t][:], s_ps[:], ACT.Exp, bias=neg_top[t][:])
-
-        def finish(first, last):
-            nc.vector.reciprocal(inv[:, first:last], total[:, first:last])
-            for t in range(first, last):
-                res = sb("res%d" % t, [P, V], F32)
-                nc.vector.tensor_scalar(res[:], num[t][:], inv[:, t : t + 1], None, ALU.mult)
-                nc.sync.dma_start(out=out[t * P : (t + 1) * P, :], in_=res[:])
+            total = sb("total%d" % t, [P, 1], F32)
+            nc.scalar.activation(ex[:], y_ps[t][:], ACT.Exp, bias=neg_top[t][:], accum_out=total[:])
+            num = sb("num%d" % t, [P, V], F32)
+            nc.scalar.activation(num[:], s_ps[:], ACT.Exp, bias=neg_top[t][:])
+            inv = sb("inv%d" % t, [P, 1], F32)
+            res = sb("res%d" % t, [P, V], F32)
+            if t < 2:
+                nc.gpsimd.tensor_tensor(inv[:], total[:], minus_one[:], ALU.pow)
+                nc.gpsimd.tensor_scalar(res[:], num[:], inv[:], 0.0, ALU.mult, ALU.add)
+            else:
+                nc.vector.reciprocal(inv[:], total[:])
+                nc.vector.tensor_scalar(res[:], num[:], inv[:], None, ALU.mult)
+            nc.sync.dma_start(out=out[t * P : (t + 1) * P, :], in_=res[:])
 
         for t in range(TILES):
             project(t)
@@ -222,14 +222,11 @@ def tile_picked_yqbn_norm_p_kernel(
         row_max(0)
         nc.vector.tensor_copy(d_g[:], dw_win[:].indirect(qry_t[:]))
         row_max(1)
-        exps(0)
+        finish(0)
         quant_h(3)
         bank_scores(3)
-        exps(1)
+        finish(1)
         row_max(2)
         row_max(3)
-        exps(2)
-        exps(3)
-        finish(0, 2)
-        finish(2, 3)
-        finish(3, 4)
+        finish(2)
+        finish(3)

@@ -135,9 +135,10 @@ def tile_picked_yqbn_norm_p_kernel(
                 rhs=x0_g[:].bitcast(FP8X4), rhs_scale=es_g[E_ROW:P, :], start=True, stop=True,
             )
         weave_w(nc.scalar.copy, w1a, 1, 0, 64)
-        weave_w(nc.scalar.copy, w1b, 1, 64, P, 64)
+        weave_w(nc.scalar.copy, w1b, 1, 64, 88, 64)
+        weave_w(nc.vector.tensor_copy, w1b, 1, 88, P, 64)
         quant_w(1)
-        x1_first = sb("x1_first", [P, P], U32)
+        x1_first = at("x1_first", 7 * kb, [P, P], U32)
         x1_rest = at("x1_rest", 4 * kb, [P, S - P], U32)
         nc.vector.tensor_copy(x1_first[:], x1_win[:].indirect(offs_t[:, 0:8]))
         nc.vector.tensor_copy(x1_rest[:], x1_win[:].indirect(offs_t[:, 8:32]))
@@ -170,7 +171,7 @@ def tile_picked_yqbn_norm_p_kernel(
 
         def quant_h(t):
             if t == 0:
-                h_codes[t] = at("h_codes0", 16 * kb, [P, P], U32)
+                h_codes[t] = at("h_codes0", 12 * kb, [P, P], U32)
             else:
                 h_codes[t] = at("h_codes%d" % t, 16 * kb + 512 * t, [P, P], U32)
             h_sc[t] = sb("h_sc%d" % t, [P, P], U8)

@@ -84,6 +84,11 @@ def tile_picked_yqbn_norm_p_kernel(
                 out=w_codes[o][:].bitcast(FP8X4), scales=w_sc[o][:], in_=w_bf[o][:].rearrange("p t m j -> p (t m j)")
             )
 
+        ds_win = sb("ds_win", [P, G], U8)
+        nc.gpsimd.memset(ds_win[:].bitcast(I32), 0)
+        for q in QUADS:
+            load_scales(nc.gpsimd, ds_win, D_ROW, d_scales, q)
+
         xs_g = sb("xs_g", [P, S], U8)
         es_g = sb("es_g", [P, U], U8)
         d_g = sb("d_g", [P, V], U32)
@@ -112,10 +117,6 @@ def tile_picked_yqbn_norm_p_kernel(
         x1_win = at("x1_win", 8 * kb, [P, T], U32)
         load_w(w1b[:], w_rows[1][:, :, H // 2 : H])
         load_words(x1_win[:], x_words[1])
-        ds_win = at("ds_win", 12 * kb, [P, G], U8)
-        nc.gpsimd.memset(ds_win[:].bitcast(I32), 0)
-        for q in QUADS:
-            load_scales(nc.sync, ds_win, D_ROW, d_scales, q)
 
         nc.vector.tensor_copy(es_g[:], es_win.indirect(bank_t[:]))
         ew_win = at("ew_win", 16 * kb, [P, W], U32)
@@ -135,8 +136,8 @@ def tile_picked_yqbn_norm_p_kernel(
                 rhs=x0_g[:].bitcast(FP8X4), rhs_scale=es_g[E_ROW:P, :], start=True, stop=True,
             )
         weave_w(nc.scalar.copy, w1a, 1, 0, 64)
-        weave_w(nc.scalar.copy, w1b, 1, 64, 88, 64)
-        weave_w(nc.vector.tensor_copy, w1b, 1, 88, P, 64)
+        weave_w(nc.scalar.copy, w1b, 1, 64, 96, 64)
+        weave_w(nc.vector.tensor_copy, w1b, 1, 96, P, 64)
         quant_w(1)
         x1_first = at("x1_first", 7 * kb, [P, P], U32)
         x1_rest = at("x1_rest", 4 * kb, [P, S - P], U32)
@@ -171,7 +172,7 @@ def tile_picked_yqbn_norm_p_kernel(
 
         def quant_h(t):
             if t == 0:
-                h_codes[t] = at("h_codes0", 12 * kb, [P, P], U32)
+                h_codes[t] = at("h_codes0", 8 * kb, [P, P], U32)
             else:
                 h_codes[t] = at("h_codes%d" % t, 16 * kb + 512 * t, [P, P], U32)
             h_sc[t] = sb("h_sc%d" % t, [P, P], U8)

@@ -46,14 +46,14 @@ def tile_picked_yqbn_norm_p_kernel(
             return stage.tile(shape, dtype, name=name, offset=offset, align_bytes=64)
 
         kb = 1024
-        w0 = sb("w0", [P, PACK, H], F32)
+        w0 = at("w0", 44 * kb, [P, PACK, H], F32)
         x0_hold = at("x0_hold", 4 * kb, [P, 10 * kb // 4], U32)
-        es_hold = at("es_hold", 14 * kb, [P, 14 * kb], U8)
+        xs_hold = at("xs_hold", 14 * kb, [P, 14 * kb], U8)
         warm_out = at("warm_out", 36 * kb, [P, 8 * kb // 4], F32)
         x0_win = x0_hold[:, 0:T]
-        es_win = es_hold[:, 0:W]
+        xs_win = xs_hold[:, 0:T]
 
-        nc.vector.memset(es_win.bitcast(I32), 0)
+        nc.vector.memset(xs_win.bitcast(I32), 0)
         nc.vector.memset(w0[:, 3, 0:8], 0.0)
         nc.scalar.activation(warm_out[:, 0:8], w0[:, 3, 0:8], ACT.Exp)
 
@@ -84,13 +84,7 @@ def tile_picked_yqbn_norm_p_kernel(
                 out=w_codes[o][:].bitcast(FP8X4), scales=w_sc[o][:], in_=w_bf[o][:].rearrange("p t m j -> p (t m j)")
             )
 
-        ds_win = sb("ds_win", [P, G], U8)
-        nc.gpsimd.memset(ds_win[:].bitcast(I32), 0)
-        for q in QUADS:
-            load_scales(nc.gpsimd, ds_win, D_ROW, d_scales, q)
-
         xs_g = sb("xs_g", [P, S], U8)
-        es_g = sb("es_g", [P, U], U8)
         d_g = sb("d_g", [P, V], U32)
         e_g = sb("e_g", [P, U], U32)
 
@@ -101,15 +95,15 @@ def tile_picked_yqbn_norm_p_kernel(
         nc.sync.dma_start(qry_t[:], qry)
         load_w(w0[:, 0:2, :], w_rows[0][:, 0:2, :])
         for q in QUADS:
-            load_scales(nc.sync, es_win, E_ROW, e_scales, q)
+            load_scales(nc.sync, xs_win, 0, x_scales, q)
 
         load_w(w0[:, 2:4, :], w_rows[0][:, 2:4, :])
         w1a = at("w1a", 40 * kb, [P, PACK, H // 2], F32)
         load_w(w1a[:], w_rows[1][:, :, 0 : H // 2])
-        xs_win = at("xs_win", 36 * kb, [P, T], U8)
-        nc.vector.memset(xs_win[:].bitcast(I32), 0)
+        ds_win = at("ds_win", 36 * kb, [P, G], U8)
+        nc.vector.memset(ds_win[:].bitcast(I32), 0)
         for q in QUADS:
-            load_scales(nc.sync, xs_win, 0, x_scales, q)
+            load_scales(nc.sync, ds_win, D_ROW, d_scales, q)
 
         x0_g = at("x0_g", 38 * kb, [P, S], U32)
         nc.vector.tensor_copy(x0_g[:], x0_win.indirect(offs_t[:]))
@@ -117,8 +111,12 @@ def tile_picked_yqbn_norm_p_kernel(
         x1_win = at("x1_win", 8 * kb, [P, T], U32)
         load_w(w1b[:], w_rows[1][:, :, H // 2 : H])
         load_words(x1_win[:], x_words[1])
+        es_win = at("es_win", 12 * kb, [P, W], U8)
+        nc.gpsimd.memset(es_win[:].bitcast(I32), 0)
+        for q in QUADS:
+            load_scales(nc.sync, es_win, E_ROW, e_scales, q)
 
-        nc.vector.tensor_copy(es_g[:], es_win.indirect(bank_t[:]))
+        nc.vector.tensor_copy(xs_g[:], xs_win.indirect(offs_t[:]))
         ew_win = at("ew_win", 16 * kb, [P, W], U32)
         dw_win = at("dw_win", 24 * kb, [P, G], U32)
         load_words(ew_win[:], e_words[0])
@@ -127,13 +125,14 @@ def tile_picked_yqbn_norm_p_kernel(
         weave_w(nc.scalar.copy, w0, 0, 0, 56)
         weave_w(nc.vector.tensor_copy, w0, 0, 56, P)
         quant_w(0)
-        nc.vector.tensor_copy(xs_g[:], xs_win[:].indirect(offs_t[:]))
+        ds_g = at("ds_g", 44 * kb, [P, V], U8)
+        nc.vector.tensor_copy(ds_g[:], ds_win[:].indirect(qry_t[:]))
         warm_ps = psum_y.tile([P, U], F32, name="y_ps")
-        for j in range(3):
+        for j in range(2):
             nc.tensor.matmul_mx(
                 out=warm_ps[:], lhsT=w_codes[0][:, j * P : (j + 1) * P].bitcast(FP8X4),
                 lhsT_scale=w_sc[0][:, j * P : (j + 1) * P],
-                rhs=x0_g[:].bitcast(FP8X4), rhs_scale=es_g[E_ROW:P, :], start=True, stop=True,
+                rhs=x0_g[:].bitcast(FP8X4), rhs_scale=xs_g[:], start=True, stop=True,
             )
         weave_w(nc.scalar.copy, w1a, 1, 0, 64)
         weave_w(nc.scalar.copy, w1b, 1, 64, 96, 64)
@@ -144,13 +143,17 @@ def tile_picked_yqbn_norm_p_kernel(
         nc.vector.tensor_copy(x1_first[:], x1_win[:].indirect(offs_t[:, 0:8]))
         nc.vector.tensor_copy(x1_rest[:], x1_win[:].indirect(offs_t[:, 8:32]))
         x1_g = [x1_first[:]] + [x1_rest[:, (t - 1) * P : t * P] for t in range(1, TILES)]
-        ds_g = at("ds_g", 6 * kb, [P, V], U8)
-        nc.vector.tensor_copy(ds_g[:], ds_win[:].indirect(qry_t[:]))
 
-        minus_one = sb("minus_one", [P, 1], F32)
-        nc.gpsimd.memset(minus_one[:], -1.0)
-
-        h_bf, h_codes, h_sc, y_ps, neg_top = {}, {}, {}, {}, {}
+        h0_bf = sb("h0_bf", [P, P, PACK], BF16)
+        h1_bf = sb("h1_bf", [P, P, PACK], BF16)
+        h23_bf = sb("h23_bf", [P, 2, P, PACK], BF16)
+        h_bf = [h0_bf[:], h1_bf[:], h23_bf[:, 0], h23_bf[:, 1]]
+        h_src = {
+            0: h0_bf[:].rearrange("p t j -> p (t j)"),
+            1: h1_bf[:].rearrange("p t j -> p (t j)"),
+            2: h23_bf[:].rearrange("p u t j -> p (u t j)"),
+        }
+        h_codes, h_sc, y_ps, neg_top = {}, {}, {}, {}
 
         def project(t):
             cols = slice(t * P, (t + 1) * P)
@@ -167,23 +170,19 @@ def tile_picked_yqbn_norm_p_kernel(
                         start=(o == 0),
                         stop=(o == PASSES - 1),
                     )
-            h_bf[t] = sb("h_bf%d" % t, [P, P, PACK], BF16)
-            nc.scalar.copy(h_bf[t][:], h_ps[:].rearrange("p j t -> p t j"))
+            nc.scalar.copy(h_bf[t], h_ps[:].rearrange("p j t -> p t j"))
 
-        def quant_h(t):
-            if t == 0:
-                h_codes[t] = at("h_codes0", 8 * kb, [P, P], U32)
-            else:
-                h_codes[t] = at("h_codes%d" % t, 16 * kb + 512 * t, [P, P], U32)
-            h_sc[t] = sb("h_sc%d" % t, [P, P], U8)
-            nc.vector.quantize_mx(
-                out=h_codes[t][:].bitcast(FP8X4), scales=h_sc[t][:], in_=h_bf[t][:].rearrange("p t j -> p (t j)")
-            )
+        def quant_h(first, count, codes):
+            scales = sb("h_sc%d" % first, [P, count * P], U8)
+            nc.vector.quantize_mx(out=codes[:].bitcast(FP8X4), scales=scales[:], in_=h_src[first])
+            for u in range(count):
+                h_codes[first + u] = codes[:, u * P : (u + 1) * P]
+                h_sc[first + u] = scales[:, u * P : (u + 1) * P]
 
         def bank_scores(t):
             y_ps[t] = psum_y.tile([P, U], F32, name="y_ps")
             nc.tensor.matmul_mx(
-                out=y_ps[t][:], lhsT=h_codes[t][:].bitcast(FP8X4), lhsT_scale=h_sc[t][:],
+                out=y_ps[t][:], lhsT=h_codes[t].bitcast(FP8X4), lhsT_scale=h_sc[t],
                 rhs=e_g[:].bitcast(FP8X4), rhs_scale=es_g[E_ROW:P, :], start=True, stop=True,
             )
 
@@ -191,44 +190,46 @@ def tile_picked_yqbn_norm_p_kernel(
             neg_top[t] = sb("neg_top%d" % t, [P, 1], F32)
             nc.vector.tensor_reduce(neg_top[t][:], y_ps[t][:], AX.X, ALU.max, negate=True)
 
+        total = sb("total", [P, TILES], F32)
+        inv = sb("inv", [P, TILES], F32)
+
+        def bank_sum(t):
+            ex = sb("ex%d" % t, [P, U], F32)
+            nc.scalar.activation(ex[:], y_ps[t][:], ACT.Exp, bias=neg_top[t][:], accum_out=total[:, t : t + 1])
+
         def finish(t):
             s_ps = psum_h.tile([P, V], F32, name="h_ps")
             nc.tensor.matmul_mx(
-                out=s_ps[:], lhsT=h_codes[t][:].bitcast(FP8X4), lhsT_scale=h_sc[t][:],
+                out=s_ps[:], lhsT=h_codes[t].bitcast(FP8X4), lhsT_scale=h_sc[t],
                 rhs=d_g[:].bitcast(FP8X4), rhs_scale=ds_g[D_ROW:P, :], start=True, stop=True,
             )
-            ex = sb("ex%d" % t, [P, U], F32)
-            total = sb("total%d" % t, [P, 1], F32)
-            nc.scalar.activation(ex[:], y_ps[t][:], ACT.Exp, bias=neg_top[t][:], accum_out=total[:])
             num = sb("num%d" % t, [P, V], F32)
             nc.scalar.activation(num[:], s_ps[:], ACT.Exp, bias=neg_top[t][:])
-            inv = sb("inv%d" % t, [P, 1], F32)
             res = sb("res%d" % t, [P, V], F32)
-            if t < 2:
-                nc.gpsimd.tensor_tensor(inv[:], total[:], minus_one[:], ALU.pow)
-                nc.gpsimd.tensor_scalar(res[:], num[:], inv[:], 0.0, ALU.mult, ALU.add)
-            else:
-                nc.vector.reciprocal(inv[:], total[:])
-                nc.vector.tensor_scalar(res[:], num[:], inv[:], None, ALU.mult)
+            nc.vector.tensor_scalar(res[:], num[:], inv[:, t : t + 1], None, ALU.mult)
             nc.sync.dma_start(out=out[t * P : (t + 1) * P, :], in_=res[:])
 
-        for t in range(TILES):
+        project(0)
+        es_g = at("es_g", 34 * kb, [P, U], U8)
+        nc.vector.tensor_copy(es_g[:], es_win[:].indirect(bank_t[:]))
+        for t in range(1, TILES):
             project(t)
         nc.vector.tensor_copy(e_g[:], ew_win[:].indirect(bank_t[:]))
-        quant_h(0)
+        nc.tensor.matmul_mx(
+            out=warm_ps[:], lhsT=w_codes[0][:, 0:P].bitcast(FP8X4), lhsT_scale=w_sc[0][:, 0:P],
+            rhs=e_g[:].bitcast(FP8X4), rhs_scale=es_g[E_ROW:P, :], start=True, stop=True,
+        )
+        quant_h(0, 1, at("h_codes0", 18 * kb, [P, P], U32))
         bank_scores(0)
-        quant_h(1)
+        quant_h(1, 1, at("h_codes1", 19 * kb, [P, P], U32))
         bank_scores(1)
-        quant_h(2)
+        quant_h(2, 2, at("h_codes2", 16 * kb, [P, 2 * P], U32))
         bank_scores(2)
-        row_max(0)
-        nc.vector.tensor_copy(d_g[:], dw_win[:].indirect(qry_t[:]))
-        row_max(1)
-        finish(0)
-        quant_h(3)
         bank_scores(3)
-        finish(1)
-        row_max(2)
-        row_max(3)
-        finish(2)
-        finish(3)
+        for t in range(TILES):
+            row_max(t)
+            bank_sum(t)
+        nc.vector.tensor_copy(d_g[:], dw_win[:].indirect(qry_t[:]))
+        nc.vector.reciprocal(inv[:], total[:])
+        for t in range(TILES):
+            finish(t)

@@ -49,13 +49,14 @@ def tile_picked_yqbn_norm_p_kernel(
         w0 = at("w0", 44 * kb, [P, PACK, H], F32)
         x0_hold = at("x0_hold", 4 * kb, [P, 10 * kb // 4], U32)
         xs_hold = at("xs_hold", 14 * kb, [P, 14 * kb], U8)
-        warm_out = at("warm_out", 36 * kb, [P, 8 * kb // 4], F32)
         x0_win = x0_hold[:, 0:T]
         xs_win = xs_hold[:, 0:T]
 
         nc.vector.memset(xs_win.bitcast(I32), 0)
-        nc.vector.memset(w0[:, 3, 0:8], 0.0)
-        nc.scalar.activation(warm_out[:, 0:8], w0[:, 3, 0:8], ACT.Exp)
+        ds_win = sb("ds_win", [P, G], U8)
+        es_win = sb("es_win", [P, W], U8)
+        nc.vector.memset(ds_win[:].bitcast(I32), 0)
+        nc.vector.memset(es_win[:].bitcast(I32), 0)
 
         def load_w(raw, rows):
             nc.sync.dma_start(out=raw, in_=rows)
@@ -74,9 +75,12 @@ def tile_picked_yqbn_norm_p_kernel(
         w_codes = [sb("w_codes%d" % o, [P, H], U32) for o in range(PASSES)]
         w_sc = [sb("w_sc%d" % o, [P, H], U8) for o in range(PASSES)]
 
-        def weave_w(copy, raw, o, m0, m1, first=0):
-            src = raw[:, :, PACK * (m0 - first) : PACK * (m1 - first)].rearrange("p j (m t) -> p m j t", t=PACK)
-            dst = w_bf[o][:, :, m0:m1, :].rearrange("p t m j -> p m j t")
+        def scalar_cast(dst, src):
+            nc.scalar.activation(dst, src, ACT.Copy)
+
+        def weave_w(copy, raw, o, m0, m1, first=0, j0=0, j1=PACK):
+            src = raw[:, j0:j1, PACK * (m0 - first) : PACK * (m1 - first)].rearrange("p j (m t) -> p m j t", t=PACK)
+            dst = w_bf[o][:, :, m0:m1, j0:j1].rearrange("p t m j -> p m j t")
             copy(dst, src)
 
         def quant_w(o):
@@ -85,7 +89,6 @@ def tile_picked_yqbn_norm_p_kernel(
             )
 
         xs_g = sb("xs_g", [P, S], U8)
-        d_g = sb("d_g", [P, V], U32)
         e_g = sb("e_g", [P, U], U32)
 
         w_rows = w1.rearrange("(o p j) i -> o p j i", o=PASSES, j=PACK)
@@ -100,8 +103,6 @@ def tile_picked_yqbn_norm_p_kernel(
         load_w(w0[:, 2:4, :], w_rows[0][:, 2:4, :])
         w1a = at("w1a", 40 * kb, [P, PACK, H // 2], F32)
         load_w(w1a[:], w_rows[1][:, :, 0 : H // 2])
-        ds_win = at("ds_win", 36 * kb, [P, G], U8)
-        nc.vector.memset(ds_win[:].bitcast(I32), 0)
         for q in QUADS:
             load_scales(nc.sync, ds_win, D_ROW, d_scales, q)
 
@@ -111,8 +112,6 @@ def tile_picked_yqbn_norm_p_kernel(
         x1_win = at("x1_win", 8 * kb, [P, T], U32)
         load_w(w1b[:], w_rows[1][:, :, H // 2 : H])
         load_words(x1_win[:], x_words[1])
-        es_win = at("es_win", 12 * kb, [P, W], U8)
-        nc.gpsimd.memset(es_win[:].bitcast(I32), 0)
         for q in QUADS:
             load_scales(nc.sync, es_win, E_ROW, e_scales, q)
 
@@ -122,18 +121,30 @@ def tile_picked_yqbn_norm_p_kernel(
         load_words(ew_win[:], e_words[0])
         load_words(dw_win[:], d_words[0])
 
-        weave_w(nc.scalar.copy, w0, 0, 0, 56)
-        weave_w(nc.vector.tensor_copy, w0, 0, 56, P)
+        weave_w(scalar_cast, w0, 0, 0, 16, 0, 0, 2)
+        weave_w(nc.scalar.copy, w0, 0, 0, 16, 0, 2, 4)
+        weave_w(nc.scalar.copy, w0, 0, 16, 60)
+        weave_w(nc.vector.tensor_copy, w0, 0, 60, P)
         quant_w(0)
         ds_g = at("ds_g", 44 * kb, [P, V], U8)
         nc.vector.tensor_copy(ds_g[:], ds_win[:].indirect(qry_t[:]))
-        warm_ps = psum_y.tile([P, U], F32, name="y_ps")
-        for j in range(2):
-            nc.tensor.matmul_mx(
-                out=warm_ps[:], lhsT=w_codes[0][:, j * P : (j + 1) * P].bitcast(FP8X4),
-                lhsT_scale=w_sc[0][:, j * P : (j + 1) * P],
-                rhs=x0_g[:].bitcast(FP8X4), rhs_scale=xs_g[:], start=True, stop=True,
-            )
+        h_ps = [psum_h.tile([P, PACK, P], F32, name="h_ps") for t in range(TILES)]
+
+        def project(t, o, rhs):
+            cols = slice(t * P, (t + 1) * P)
+            for j in range(PACK):
+                nc.tensor.matmul_mx(
+                    out=h_ps[t][:, j, :],
+                    lhsT=w_codes[o][:, j * P : (j + 1) * P].bitcast(FP8X4),
+                    lhsT_scale=w_sc[o][:, j * P : (j + 1) * P],
+                    rhs=rhs.bitcast(FP8X4),
+                    rhs_scale=xs_g[4 * o : P, cols],
+                    start=(o == 0 and j == 0),
+                    stop=(o == PASSES - 1 and j == PACK - 1),
+                )
+
+        for t in range(TILES):
+            project(t, 0, x0_g[:, t * P : (t + 1) * P])
         weave_w(nc.scalar.copy, w1a, 1, 0, 64)
         weave_w(nc.scalar.copy, w1b, 1, 64, 96, 64)
         weave_w(nc.vector.tensor_copy, w1b, 1, 96, P, 64)
@@ -155,22 +166,9 @@ def tile_picked_yqbn_norm_p_kernel(
         }
         h_codes, h_sc, y_ps, neg_top = {}, {}, {}, {}
 
-        def project(t):
-            cols = slice(t * P, (t + 1) * P)
-            h_ps = psum_h.tile([P, PACK, P], F32, name="h_ps")
-            for j in range(PACK):
-                for o in range(PASSES):
-                    rhs = x0_g[:, cols] if o == 0 else x1_g[t]
-                    nc.tensor.matmul_mx(
-                        out=h_ps[:, j, :],
-                        lhsT=w_codes[o][:, j * P : (j + 1) * P].bitcast(FP8X4),
-                        lhsT_scale=w_sc[o][:, j * P : (j + 1) * P],
-                        rhs=rhs.bitcast(FP8X4),
-                        rhs_scale=xs_g[4 * o : P, cols],
-                        start=(o == 0),
-                        stop=(o == PASSES - 1),
-                    )
-            nc.scalar.copy(h_bf[t], h_ps[:].rearrange("p j t -> p t j"))
+        def close_h(t):
+            project(t, 1, x1_g[t])
+            nc.scalar.copy(h_bf[t], h_ps[t][:].rearrange("p j t -> p t j"))
 
         def quant_h(first, count, codes):
             scales = sb("h_sc%d" % first, [P, count * P], U8)
@@ -190,35 +188,45 @@ def tile_picked_yqbn_norm_p_kernel(
             neg_top[t] = sb("neg_top%d" % t, [P, 1], F32)
             nc.vector.tensor_reduce(neg_top[t][:], y_ps[t][:], AX.X, ALU.max, negate=True)
 
-        total = sb("total", [P, TILES], F32)
-        inv = sb("inv", [P, TILES], F32)
+        total = [sb("total%d" % u, [P, 2], F32) for u in range(2)]
+        inv = [sb("inv%d" % u, [P, 2], F32) for u in range(2)]
 
         def bank_sum(t):
             ex = sb("ex%d" % t, [P, U], F32)
-            nc.scalar.activation(ex[:], y_ps[t][:], ACT.Exp, bias=neg_top[t][:], accum_out=total[:, t : t + 1])
+            nc.scalar.activation(ex[:], y_ps[t][:], ACT.Exp, bias=neg_top[t][:], accum_out=total[t // 2][:, t % 2 : t % 2 + 1])
+
+        s_ps = {}
+        num = [sb("num%d" % t, [P, V], F32) for t in range(TILES)]
+        HALF = V // 2
+
+        def query_scores(t, c0, c1):
+            if t not in s_ps:
+                s_ps[t] = psum_h.tile([P, V], F32, name="h_ps")
+            codes = d_half[c0 // HALF] if c1 - c0 == HALF else None
+            nc.tensor.matmul_mx(
+                out=s_ps[t][:, c0:c1], lhsT=h_codes[t].bitcast(FP8X4), lhsT_scale=h_sc[t],
+                rhs=codes[:].bitcast(FP8X4), rhs_scale=ds_g[D_ROW:P, c0:c1], start=True, stop=True,
+            )
+
+        def query_exp(t, c0, c1):
+            nc.scalar.activation(num[t][:, c0:c1], s_ps[t][:, c0:c1], ACT.Exp, bias=neg_top[t][:])
 
         def finish(t):
-            s_ps = psum_h.tile([P, V], F32, name="h_ps")
-            nc.tensor.matmul_mx(
-                out=s_ps[:], lhsT=h_codes[t].bitcast(FP8X4), lhsT_scale=h_sc[t],
-                rhs=d_g[:].bitcast(FP8X4), rhs_scale=ds_g[D_ROW:P, :], start=True, stop=True,
-            )
-            num = sb("num%d" % t, [P, V], F32)
-            nc.scalar.activation(num[:], s_ps[:], ACT.Exp, bias=neg_top[t][:])
             res = sb("res%d" % t, [P, V], F32)
-            nc.vector.tensor_scalar(res[:], num[:], inv[:, t : t + 1], None, ALU.mult)
+            nc.vector.tensor_scalar(res[:], num[t][:], inv[t // 2][:, t % 2 : t % 2 + 1], None, ALU.mult)
             nc.sync.dma_start(out=out[t * P : (t + 1) * P, :], in_=res[:])
 
-        project(0)
+        d_half = [sb("d_g%d" % u, [P, HALF], U32) for u in range(2)]
+
+        def gather_d(u):
+            nc.vector.tensor_copy(d_half[u][:], dw_win[:].indirect(qry_t[:, 8 * u : 8 * u + 8]))
+
+        close_h(0)
         es_g = at("es_g", 34 * kb, [P, U], U8)
         nc.vector.tensor_copy(es_g[:], es_win[:].indirect(bank_t[:]))
         for t in range(1, TILES):
-            project(t)
+            close_h(t)
         nc.vector.tensor_copy(e_g[:], ew_win[:].indirect(bank_t[:]))
-        nc.tensor.matmul_mx(
-            out=warm_ps[:], lhsT=w_codes[0][:, 0:P].bitcast(FP8X4), lhsT_scale=w_sc[0][:, 0:P],
-            rhs=e_g[:].bitcast(FP8X4), rhs_scale=es_g[E_ROW:P, :], start=True, stop=True,
-        )
         quant_h(0, 1, at("h_codes0", 18 * kb, [P, P], U32))
         bank_scores(0)
         quant_h(1, 1, at("h_codes1", 19 * kb, [P, P], U32))
@@ -226,10 +234,29 @@ def tile_picked_yqbn_norm_p_kernel(
         quant_h(2, 2, at("h_codes2", 16 * kb, [P, 2 * P], U32))
         bank_scores(2)
         bank_scores(3)
-        for t in range(TILES):
-            row_max(t)
-            bank_sum(t)
-        nc.vector.tensor_copy(d_g[:], dw_win[:].indirect(qry_t[:]))
-        nc.vector.reciprocal(inv[:], total[:])
-        for t in range(TILES):
+        row_max(0)
+        bank_sum(0)
+        row_max(1)
+        bank_sum(1)
+        gather_d(0)
+        for t in range(2):
+            query_scores(t, 0, HALF)
+            query_exp(t, 0, HALF)
+        row_max(2)
+        bank_sum(2)
+        gather_d(1)
+        for t in range(2):
+            query_scores(t, HALF, V)
+            query_exp(t, HALF, V)
+        for t in range(2, TILES):
+            query_scores(t, 0, HALF)
+            query_scores(t, HALF, V)
+        row_max(3)
+        bank_sum(3)
+        nc.vector.reciprocal(inv[0][:], total[0][:])
+        finish(0)
+        finish(1)
+        nc.vector.reciprocal(inv[1][:], total[1][:])
+        for t in range(2, TILES):
+            query_exp(t, 0, V)
             finish(t)

@@ -47,16 +47,18 @@ def tile_picked_yqbn_norm_p_kernel(
 
         kb = 1024
         w0 = at("w0", 44 * kb, [P, PACK, H], F32)
-        x0_hold = at("x0_hold", 4 * kb, [P, 10 * kb // 4], U32)
-        xs_hold = at("xs_hold", 14 * kb, [P, 14 * kb], U8)
-        x0_win = x0_hold[:, 0:T]
-        xs_win = xs_hold[:, 0:T]
+        x0_win = sb("x0_win", [P, T], U32)[:]
+        xs_win = sb("xs_win", [P, T], U8)[:]
 
         nc.vector.memset(xs_win.bitcast(I32), 0)
+        warm_in = sb("warm_in", [P, 8], F32)
+        warm_out = sb("warm_out", [P, 8], F32)
+        nc.vector.memset(warm_in[:], 0.0)
+        nc.scalar.activation(warm_out[:], warm_in[:], ACT.Exp)
         ds_win = sb("ds_win", [P, G], U8)
         es_win = sb("es_win", [P, W], U8)
-        nc.vector.memset(ds_win[:].bitcast(I32), 0)
         nc.vector.memset(es_win[:].bitcast(I32), 0)
+        nc.vector.memset(ds_win[:].bitcast(I32), 0)
 
         def load_w(raw, rows):
             nc.sync.dma_start(out=raw, in_=rows)
@@ -75,9 +77,6 @@ def tile_picked_yqbn_norm_p_kernel(
         w_codes = [sb("w_codes%d" % o, [P, H], U32) for o in range(PASSES)]
         w_sc = [sb("w_sc%d" % o, [P, H], U8) for o in range(PASSES)]
 
-        def scalar_cast(dst, src):
-            nc.scalar.activation(dst, src, ACT.Copy)
-
         def weave_w(copy, raw, o, m0, m1, first=0, j0=0, j1=PACK):
             src = raw[:, j0:j1, PACK * (m0 - first) : PACK * (m1 - first)].rearrange("p j (m t) -> p m j t", t=PACK)
             dst = w_bf[o][:, :, m0:m1, j0:j1].rearrange("p t m j -> p m j t")
@@ -92,42 +91,37 @@ def tile_picked_yqbn_norm_p_kernel(
         e_g = sb("e_g", [P, U], U32)
 
         w_rows = w1.rearrange("(o p j) i -> o p j i", o=PASSES, j=PACK)
+        w1a = sb("w1a", [P, PACK, H // 2], F32)
+        w1b = sb("w1b", [P, PACK, H // 2], F32)
+        x1_win = sb("x1_win", [P, T], U32)
+        ew_win = at("ew_win", 16 * kb, [P, W], U32)
+        dw_win = sb("dw_win", [P, G], U32)
+        x0_g = sb("x0_g", [P, S], U32)
         nc.sync.dma_start(offs_t[:], offs)
-        nc.sync.dma_start(bank_t[:], bank)
         load_words(x0_win, x_words[0])
-        nc.sync.dma_start(qry_t[:], qry)
-        load_w(w0[:, 0:2, :], w_rows[0][:, 0:2, :])
         for q in QUADS:
             load_scales(nc.sync, xs_win, 0, x_scales, q)
-
+        load_w(w0[:, 0:2, :], w_rows[0][:, 0:2, :])
         load_w(w0[:, 2:4, :], w_rows[0][:, 2:4, :])
-        w1a = at("w1a", 40 * kb, [P, PACK, H // 2], F32)
-        load_w(w1a[:], w_rows[1][:, :, 0 : H // 2])
-        for q in QUADS:
-            load_scales(nc.sync, ds_win, D_ROW, d_scales, q)
-
-        x0_g = at("x0_g", 38 * kb, [P, S], U32)
-        nc.vector.tensor_copy(x0_g[:], x0_win.indirect(offs_t[:]))
-        w1b = at("w1b", 4 * kb, [P, PACK, H // 2], F32)
-        x1_win = at("x1_win", 8 * kb, [P, T], U32)
-        load_w(w1b[:], w_rows[1][:, :, H // 2 : H])
-        load_words(x1_win[:], x_words[1])
+        nc.sync.dma_start(bank_t[:], bank)
         for q in QUADS:
             load_scales(nc.sync, es_win, E_ROW, e_scales, q)
-
-        nc.vector.tensor_copy(xs_g[:], xs_win.indirect(offs_t[:]))
-        ew_win = at("ew_win", 16 * kb, [P, W], U32)
-        dw_win = at("dw_win", 24 * kb, [P, G], U32)
+        load_w(w1a[:], w_rows[1][:, :, 0 : H // 2])
+        load_w(w1b[:], w_rows[1][:, :, H // 2 : H])
+        nc.sync.dma_start(qry_t[:], qry)
+        for q in QUADS:
+            load_scales(nc.sync, ds_win, D_ROW, d_scales, q)
+        load_words(x1_win[:], x_words[1])
         load_words(ew_win[:], e_words[0])
         load_words(dw_win[:], d_words[0])
 
-        weave_w(scalar_cast, w0, 0, 0, 16, 0, 0, 2)
-        weave_w(nc.scalar.copy, w0, 0, 0, 16, 0, 2, 4)
-        weave_w(nc.scalar.copy, w0, 0, 16, 60)
-        weave_w(nc.vector.tensor_copy, w0, 0, 60, P)
+        nc.vector.tensor_copy(x0_g[:], x0_win.indirect(offs_t[:]))
+        nc.vector.tensor_copy(xs_g[:], xs_win.indirect(offs_t[:]))
+        weave_w(nc.scalar.copy, w0, 0, 0, 48)
+        weave_w(nc.vector.tensor_copy, w0, 0, 48, P)
         quant_w(0)
-        ds_g = at("ds_g", 44 * kb, [P, V], U8)
-        nc.vector.tensor_copy(ds_g[:], ds_win[:].indirect(qry_t[:]))
+        es_g = sb("es_g", [P, U], U8)
+        nc.vector.tensor_copy(es_g[:], es_win[:].indirect(bank_t[:]))
         h_ps = [psum_h.tile([P, PACK, P], F32, name="h_ps") for t in range(TILES)]
 
         def project(t, o, rhs):
@@ -149,20 +143,18 @@ def tile_picked_yqbn_norm_p_kernel(
         weave_w(nc.scalar.copy, w1b, 1, 64, 96, 64)
         weave_w(nc.vector.tensor_copy, w1b, 1, 96, P, 64)
         quant_w(1)
-        x1_first = at("x1_first", 7 * kb, [P, P], U32)
-        x1_rest = at("x1_rest", 4 * kb, [P, S - P], U32)
-        nc.vector.tensor_copy(x1_first[:], x1_win[:].indirect(offs_t[:, 0:8]))
-        nc.vector.tensor_copy(x1_rest[:], x1_win[:].indirect(offs_t[:, 8:32]))
-        x1_g = [x1_first[:]] + [x1_rest[:, (t - 1) * P : t * P] for t in range(1, TILES)]
+        x1_cuts = (0, P, 2 * P, S)
+        x1_part = [at("x1_part0", 0, [P, P], U32), sb("x1_part1", [P, P], U32), sb("x1_part2", [P, 2 * P], U32)]
+        for u in range(3):
+            nc.vector.tensor_copy(x1_part[u][:], x1_win[:].indirect(offs_t[:, x1_cuts[u] // 16 : x1_cuts[u + 1] // 16]))
+        x1_g = [x1_part[0][:], x1_part[1][:], x1_part[2][:, 0:P], x1_part[2][:, P : 2 * P]]
 
         h0_bf = sb("h0_bf", [P, P, PACK], BF16)
-        h1_bf = sb("h1_bf", [P, P, PACK], BF16)
-        h23_bf = sb("h23_bf", [P, 2, P, PACK], BF16)
-        h_bf = [h0_bf[:], h1_bf[:], h23_bf[:, 0], h23_bf[:, 1]]
+        rest_bf = sb("rest_bf", [P, 3, P, PACK], BF16)
+        h_bf = [h0_bf[:], rest_bf[:, 0], rest_bf[:, 1], rest_bf[:, 2]]
         h_src = {
             0: h0_bf[:].rearrange("p t j -> p (t j)"),
-            1: h1_bf[:].rearrange("p t j -> p (t j)"),
-            2: h23_bf[:].rearrange("p u t j -> p (u t j)"),
+            1: rest_bf[:].rearrange("p u t j -> p (u t j)"),
         }
         h_codes, h_sc, y_ps, neg_top = {}, {}, {}, {}
 
@@ -188,75 +180,43 @@ def tile_picked_yqbn_norm_p_kernel(
             neg_top[t] = sb("neg_top%d" % t, [P, 1], F32)
             nc.vector.tensor_reduce(neg_top[t][:], y_ps[t][:], AX.X, ALU.max, negate=True)
 
-        total = [sb("total%d" % u, [P, 2], F32) for u in range(2)]
-        inv = [sb("inv%d" % u, [P, 2], F32) for u in range(2)]
+        total = sb("total", [P, TILES], F32)
+        inv = sb("inv", [P, TILES], F32)
 
         def bank_sum(t):
             ex = sb("ex%d" % t, [P, U], F32)
-            nc.scalar.activation(ex[:], y_ps[t][:], ACT.Exp, bias=neg_top[t][:], accum_out=total[t // 2][:, t % 2 : t % 2 + 1])
-
-        s_ps = {}
-        num = [sb("num%d" % t, [P, V], F32) for t in range(TILES)]
-        HALF = V // 2
-
-        def query_scores(t, c0, c1):
-            if t not in s_ps:
-                s_ps[t] = psum_h.tile([P, V], F32, name="h_ps")
-            codes = d_half[c0 // HALF] if c1 - c0 == HALF else None
-            nc.tensor.matmul_mx(
-                out=s_ps[t][:, c0:c1], lhsT=h_codes[t].bitcast(FP8X4), lhsT_scale=h_sc[t],
-                rhs=codes[:].bitcast(FP8X4), rhs_scale=ds_g[D_ROW:P, c0:c1], start=True, stop=True,
-            )
-
-        def query_exp(t, c0, c1):
-            nc.scalar.activation(num[t][:, c0:c1], s_ps[t][:, c0:c1], ACT.Exp, bias=neg_top[t][:])
+            nc.scalar.activation(ex[:], y_ps[t][:], ACT.Exp, bias=neg_top[t][:], accum_out=total[:, t : t + 1])
 
         def finish(t):
+            s_ps = psum_h.tile([P, V], F32, name="h_ps")
+            nc.tensor.matmul_mx(
+                out=s_ps[:], lhsT=h_codes[t].bitcast(FP8X4), lhsT_scale=h_sc[t],
+                rhs=d_g[:].bitcast(FP8X4), rhs_scale=ds_g[D_ROW:P, :], start=True, stop=True,
+            )
+            num = sb("num%d" % t, [P, V], F32)
+            nc.scalar.activation(num[:], s_ps[:], ACT.Exp, bias=neg_top[t][:])
             res = sb("res%d" % t, [P, V], F32)
-            nc.vector.tensor_scalar(res[:], num[t][:], inv[t // 2][:, t % 2 : t % 2 + 1], None, ALU.mult)
+            nc.vector.tensor_scalar(res[:], num[:], inv[:, t : t + 1], None, ALU.mult)
             nc.sync.dma_start(out=out[t * P : (t + 1) * P, :], in_=res[:])
 
-        d_half = [sb("d_g%d" % u, [P, HALF], U32) for u in range(2)]
-
-        def gather_d(u):
-            nc.vector.tensor_copy(d_half[u][:], dw_win[:].indirect(qry_t[:, 8 * u : 8 * u + 8]))
-
+        d_g = sb("d_g", [P, V], U32)
         close_h(0)
-        es_g = at("es_g", 34 * kb, [P, U], U8)
-        nc.vector.tensor_copy(es_g[:], es_win[:].indirect(bank_t[:]))
+        ds_g = at("ds_g", 0, [P, V], U8)
+        nc.vector.tensor_copy(ds_g[:], ds_win[:].indirect(qry_t[:]))
         for t in range(1, TILES):
             close_h(t)
+        quant_h(0, 1, sb("h_codes0", [P, P], U32))
         nc.vector.tensor_copy(e_g[:], ew_win[:].indirect(bank_t[:]))
-        quant_h(0, 1, at("h_codes0", 18 * kb, [P, P], U32))
         bank_scores(0)
-        quant_h(1, 1, at("h_codes1", 19 * kb, [P, P], U32))
-        bank_scores(1)
-        quant_h(2, 2, at("h_codes2", 16 * kb, [P, 2 * P], U32))
-        bank_scores(2)
-        bank_scores(3)
+        quant_h(1, 3, sb("h_codes1", [P, 3 * P], U32))
+        for t in range(1, TILES):
+            bank_scores(t)
         row_max(0)
         bank_sum(0)
-        row_max(1)
-        bank_sum(1)
-        gather_d(0)
-        for t in range(2):
-            query_scores(t, 0, HALF)
-            query_exp(t, 0, HALF)
-        row_max(2)
-        bank_sum(2)
-        gather_d(1)
-        for t in range(2):
-            query_scores(t, HALF, V)
-            query_exp(t, HALF, V)
-        for t in range(2, TILES):
-            query_scores(t, 0, HALF)
-            query_scores(t, HALF, V)
-        row_max(3)
-        bank_sum(3)
-        nc.vector.reciprocal(inv[0][:], total[0][:])
-        finish(0)
-        finish(1)
-        nc.vector.reciprocal(inv[1][:], total[1][:])
-        for t in range(2, TILES):
-            query_exp(t, 0, V)
+        for t in range(1, TILES):
+            row_max(t)
+            bank_sum(t)
+        nc.vector.tensor_copy(d_g[:], dw_win[:].indirect(qry_t[:]))
+        nc.vector.reciprocal(inv[:], total[:])
+        for t in range(TILES):
             finish(t)

@@ -20,9 +20,12 @@ P = 128
 PACK = 4
 PASSES = K // (P * PACK)
 TILES = S // P
+LIST = 16
 E_ROW = 8
 D_ROW = 12
-QUADS = (0, 2, 1, 3)
+QUADRANTS = (0, 2, 1, 3)
+SCALAR_QUADS_0 = 48
+SCALAR_QUADS_1 = 96
 
 
 def tile_picked_yqbn_norm_p_kernel(
@@ -31,143 +34,134 @@ def tile_picked_yqbn_norm_p_kernel(
     nc = tc.nc
     with ExitStack() as ctx:
         keep = ctx.enter_context(tc.tile_pool(name="keep", bufs=1))
-        psum_h = ctx.enter_context(tc.psum_pool(name="psum_h", bufs=4))
-        psum_y = ctx.enter_context(tc.psum_pool(name="psum_y", bufs=4))
+        psum_h = ctx.enter_context(tc.psum_pool(name="psum_h", bufs=TILES))
+        psum_y = ctx.enter_context(tc.psum_pool(name="psum_y", bufs=TILES))
 
-        def sb(name, shape, dtype):
-            return keep.tile(shape, dtype, name=name, align_bytes=64)
+        def sb(name, shape, dtype, tag=None):
+            return keep.tile(shape, dtype, name=name, tag=tag or name, align_bytes=64)
 
-        offs_t = sb("offs_t", [P, S // 16], U16)
-        bank_t = sb("bank_t", [P, U // 16], U16)
-        qry_t = sb("qry_t", [P, V // 16], U16)
-        stage = ctx.enter_context(tc.tile_pool(name="stage", bufs=1))
+        offs_t = sb("offs_t", [P, S // LIST], U16)
+        bank_t = sb("bank_t", [P, U // LIST], U16)
+        qry_t = sb("qry_t", [P, V // LIST], U16)
 
-        def at(name, offset, shape, dtype):
-            return stage.tile(shape, dtype, name=name, offset=offset, align_bytes=64)
-
-        kb = 1024
-        w0 = at("w0", 44 * kb, [P, PACK, H], F32)
-        x0_win = sb("x0_win", [P, T], U32)[:]
-        xs_win = sb("xs_win", [P, T], U8)[:]
-
-        nc.vector.memset(xs_win.bitcast(I32), 0)
+        xs_win = sb("xs_win", [P, T], U8)
+        es_win = sb("es_win", [P, W], U8)
+        ds_win = sb("ds_win", [P, G], U8)
+        nc.vector.memset(xs_win[:].bitcast(I32), 0)
         warm_in = sb("warm_in", [P, 8], F32)
         warm_out = sb("warm_out", [P, 8], F32)
         nc.vector.memset(warm_in[:], 0.0)
         nc.scalar.activation(warm_out[:], warm_in[:], ACT.Exp)
-        ds_win = sb("ds_win", [P, G], U8)
-        es_win = sb("es_win", [P, W], U8)
         nc.vector.memset(es_win[:].bitcast(I32), 0)
         nc.vector.memset(ds_win[:].bitcast(I32), 0)
 
-        def load_w(raw, rows):
-            nc.sync.dma_start(out=raw, in_=rows)
-
         def load_words(win, words):
-            nc.sync.dma_start(out=win.bitcast(I32), in_=words.rearrange("p n t -> p (n t)").bitcast(I32))
+            nc.sync.dma_start(out=win[:].bitcast(I32), in_=words.rearrange("p n t -> p (n t)").bitcast(I32))
 
-        def load_scales(queue, win, row, scales, q):
-            n = scales.shape[0] * 4
-            queue.dma_start(
-                out=win[32 * q + row : 32 * q + row + n, :].bitcast(I32),
-                in_=scales[:, 4 * q : 4 * q + 4, :].bitcast(I32),
-            )
+        def load_scales(win, row, scales):
+            rows = scales.shape[0] * 4
+            for q in QUADRANTS:
+                nc.sync.dma_start(
+                    out=win[32 * q + row : 32 * q + row + rows, :].bitcast(I32),
+                    in_=scales[:, 4 * q : 4 * q + 4, :].bitcast(I32),
+                )
 
-        w_bf = [at("w_bf%d" % o, (28 + 4 * o) * kb, [P, PACK, P, PACK], BF16) for o in range(PASSES)]
+        w_rows = w1.rearrange("(o p j) i -> o p j i", o=PASSES, j=PACK)
+        w0_raw = sb("w0_raw", [P, PACK, H], F32)
+        w1_left = sb("w1_left", [P, PACK, H // 2], F32)
+        w1_right = sb("w1_right", [P, PACK, H // 2], F32)
+        x_win = [sb("x_win%d" % o, [P, T], U32) for o in range(PASSES)]
+        e_win = sb("e_win", [P, W], U32)
+        d_win = sb("d_win", [P, G], U32)
+        nc.sync.dma_start(offs_t[:], offs)
+        load_words(x_win[0], x_words[0])
+        load_scales(xs_win, 0, x_scales)
+        nc.sync.dma_start(out=w0_raw[:, 0:2, :], in_=w_rows[0][:, 0:2, :])
+        nc.sync.dma_start(out=w0_raw[:, 2:4, :], in_=w_rows[0][:, 2:4, :])
+        nc.sync.dma_start(bank_t[:], bank)
+        load_scales(es_win, E_ROW, e_scales)
+        nc.sync.dma_start(out=w1_left[:], in_=w_rows[1][:, :, 0 : H // 2])
+        nc.sync.dma_start(out=w1_right[:], in_=w_rows[1][:, :, H // 2 : H])
+        nc.sync.dma_start(qry_t[:], qry)
+        load_scales(ds_win, D_ROW, d_scales)
+        load_words(x_win[1], x_words[1])
+        load_words(e_win, e_words[0])
+        load_words(d_win, d_words[0])
+
+        def gather(dst, win, entries, first, last):
+            nc.vector.tensor_copy(dst, win[:].indirect(entries[:, first // LIST : last // LIST]))
+
+        w_bf = [sb("w_bf%d" % o, [P, PACK, P, PACK], BF16) for o in range(PASSES)]
         w_codes = [sb("w_codes%d" % o, [P, H], U32) for o in range(PASSES)]
         w_sc = [sb("w_sc%d" % o, [P, H], U8) for o in range(PASSES)]
 
-        def weave_w(copy, raw, o, m0, m1, first=0, j0=0, j1=PACK):
-            src = raw[:, j0:j1, PACK * (m0 - first) : PACK * (m1 - first)].rearrange("p j (m t) -> p m j t", t=PACK)
-            dst = w_bf[o][:, :, m0:m1, j0:j1].rearrange("p t m j -> p m j t")
-            copy(dst, src)
+        def deal_w(copy, raw, o, m0, m1, raw_first=0):
+            src = raw[:, :, PACK * (m0 - raw_first) : PACK * (m1 - raw_first)].rearrange("p j (m c) -> p m j c", c=PACK)
+            copy(w_bf[o][:, :, m0:m1, :].rearrange("p c m j -> p m j c"), src)
 
         def quant_w(o):
             nc.vector.quantize_mx(
-                out=w_codes[o][:].bitcast(FP8X4), scales=w_sc[o][:], in_=w_bf[o][:].rearrange("p t m j -> p (t m j)")
+                out=w_codes[o][:].bitcast(FP8X4), scales=w_sc[o][:], in_=w_bf[o][:].rearrange("p c m j -> p (c m j)")
             )
 
-        xs_g = sb("xs_g", [P, S], U8)
-        e_g = sb("e_g", [P, U], U32)
-
-        w_rows = w1.rearrange("(o p j) i -> o p j i", o=PASSES, j=PACK)
-        w1a = sb("w1a", [P, PACK, H // 2], F32)
-        w1b = sb("w1b", [P, PACK, H // 2], F32)
-        x1_win = sb("x1_win", [P, T], U32)
-        ew_win = at("ew_win", 16 * kb, [P, W], U32)
-        dw_win = sb("dw_win", [P, G], U32)
-        x0_g = sb("x0_g", [P, S], U32)
-        nc.sync.dma_start(offs_t[:], offs)
-        load_words(x0_win, x_words[0])
-        for q in QUADS:
-            load_scales(nc.sync, xs_win, 0, x_scales, q)
-        load_w(w0[:, 0:2, :], w_rows[0][:, 0:2, :])
-        load_w(w0[:, 2:4, :], w_rows[0][:, 2:4, :])
-        nc.sync.dma_start(bank_t[:], bank)
-        for q in QUADS:
-            load_scales(nc.sync, es_win, E_ROW, e_scales, q)
-        load_w(w1a[:], w_rows[1][:, :, 0 : H // 2])
-        load_w(w1b[:], w_rows[1][:, :, H // 2 : H])
-        nc.sync.dma_start(qry_t[:], qry)
-        for q in QUADS:
-            load_scales(nc.sync, ds_win, D_ROW, d_scales, q)
-        load_words(x1_win[:], x_words[1])
-        load_words(ew_win[:], e_words[0])
-        load_words(dw_win[:], d_words[0])
-
-        nc.vector.tensor_copy(x0_g[:], x0_win.indirect(offs_t[:]))
-        nc.vector.tensor_copy(xs_g[:], xs_win.indirect(offs_t[:]))
-        weave_w(nc.scalar.copy, w0, 0, 0, 48)
-        weave_w(nc.vector.tensor_copy, w0, 0, 48, P)
-        quant_w(0)
-        es_g = sb("es_g", [P, U], U8)
-        nc.vector.tensor_copy(es_g[:], es_win[:].indirect(bank_t[:]))
         h_ps = [psum_h.tile([P, PACK, P], F32, name="h_ps") for t in range(TILES)]
 
         def project(t, o, rhs):
-            cols = slice(t * P, (t + 1) * P)
-            for j in range(PACK):
+            for c in range(PACK):
                 nc.tensor.matmul_mx(
-                    out=h_ps[t][:, j, :],
-                    lhsT=w_codes[o][:, j * P : (j + 1) * P].bitcast(FP8X4),
-                    lhsT_scale=w_sc[o][:, j * P : (j + 1) * P],
+                    out=h_ps[t][:, c, :],
+                    lhsT=w_codes[o][:, c * P : (c + 1) * P].bitcast(FP8X4),
+                    lhsT_scale=w_sc[o][:, c * P : (c + 1) * P],
                     rhs=rhs.bitcast(FP8X4),
-                    rhs_scale=xs_g[4 * o : P, cols],
-                    start=(o == 0 and j == 0),
-                    stop=(o == PASSES - 1 and j == PACK - 1),
+                    rhs_scale=xs_g[4 * o : P, t * P : (t + 1) * P],
+                    start=(o == 0 and c == 0),
+                    stop=(o == PASSES - 1 and c == PACK - 1),
                 )
 
+        x0_g = sb("x0_g", [P, S], U32)
+        xs_g = sb("xs_g", [P, S], U8)
+        es_g = sb("es_g", [P, U], U8)
+        gather(x0_g[:], x_win[0], offs_t, 0, S)
+        gather(xs_g[:], xs_win, offs_t, 0, S)
+        deal_w(nc.scalar.copy, w0_raw, 0, 0, SCALAR_QUADS_0)
+        deal_w(nc.vector.tensor_copy, w0_raw, 0, SCALAR_QUADS_0, P)
+        quant_w(0)
+        gather(es_g[:], es_win, bank_t, 0, U)
         for t in range(TILES):
             project(t, 0, x0_g[:, t * P : (t + 1) * P])
-        weave_w(nc.scalar.copy, w1a, 1, 0, 64)
-        weave_w(nc.scalar.copy, w1b, 1, 64, 96, 64)
-        weave_w(nc.vector.tensor_copy, w1b, 1, 96, P, 64)
-        quant_w(1)
-        x1_cuts = (0, P, 2 * P, S)
-        x1_part = [at("x1_part0", 0, [P, P], U32), sb("x1_part1", [P, P], U32), sb("x1_part2", [P, 2 * P], U32)]
-        for u in range(3):
-            nc.vector.tensor_copy(x1_part[u][:], x1_win[:].indirect(offs_t[:, x1_cuts[u] // 16 : x1_cuts[u + 1] // 16]))
-        x1_g = [x1_part[0][:], x1_part[1][:], x1_part[2][:, 0:P], x1_part[2][:, P : 2 * P]]
 
-        h0_bf = sb("h0_bf", [P, P, PACK], BF16)
-        rest_bf = sb("rest_bf", [P, 3, P, PACK], BF16)
-        h_bf = [h0_bf[:], rest_bf[:, 0], rest_bf[:, 1], rest_bf[:, 2]]
-        h_src = {
-            0: h0_bf[:].rearrange("p t j -> p (t j)"),
-            1: rest_bf[:].rearrange("p u t j -> p (u t j)"),
-        }
-        h_codes, h_sc, y_ps, neg_top = {}, {}, {}, {}
+        deal_w(nc.scalar.copy, w1_left, 1, 0, P // 2)
+        deal_w(nc.scalar.copy, w1_right, 1, P // 2, SCALAR_QUADS_1, P // 2)
+        deal_w(nc.vector.tensor_copy, w1_right, 1, SCALAR_QUADS_1, P, P // 2)
+        quant_w(1)
+        x1_first = sb("x1_first", [P, P], U32, tag="x1_first_then_ds_g")
+        x1_second = sb("x1_second", [P, P], U32)
+        x1_rest = sb("x1_rest", [P, 2 * P], U32)
+        gather(x1_first[:], x_win[1], offs_t, 0, P)
+        gather(x1_second[:], x_win[1], offs_t, P, 2 * P)
+        gather(x1_rest[:], x_win[1], offs_t, 2 * P, S)
+        x1_g = [x1_first[:], x1_second[:], x1_rest[:, 0:P], x1_rest[:, P : 2 * P]]
+
+        h_first = sb("h_first", [P, P, PACK], BF16)
+        h_rest = sb("h_rest", [P, TILES - 1, P, PACK], BF16)
+        h_bf = [h_first[:]] + [h_rest[:, t - 1] for t in range(1, TILES)]
 
         def close_h(t):
             project(t, 1, x1_g[t])
-            nc.scalar.copy(h_bf[t], h_ps[t][:].rearrange("p j t -> p t j"))
+            nc.scalar.copy(h_bf[t], h_ps[t][:].rearrange("p c s -> p s c"))
 
-        def quant_h(first, count, codes):
+        h_codes, h_sc, y_ps, neg_top = {}, {}, {}, {}
+
+        def quant_h(first, count, values):
+            codes = sb("h_codes%d" % first, [P, count * P], U32)
             scales = sb("h_sc%d" % first, [P, count * P], U8)
-            nc.vector.quantize_mx(out=codes[:].bitcast(FP8X4), scales=scales[:], in_=h_src[first])
-            for u in range(count):
-                h_codes[first + u] = codes[:, u * P : (u + 1) * P]
-                h_sc[first + u] = scales[:, u * P : (u + 1) * P]
+            nc.vector.quantize_mx(out=codes[:].bitcast(FP8X4), scales=scales[:], in_=values)
+            for n in range(count):
+                h_codes[first + n] = codes[:, n * P : (n + 1) * P]
+                h_sc[first + n] = scales[:, n * P : (n + 1) * P]
+
+        e_g = sb("e_g", [P, U], U32)
+        d_g = sb("d_g", [P, V], U32)
 
         def bank_scores(t):
             y_ps[t] = psum_y.tile([P, U], F32, name="y_ps")
@@ -176,47 +170,48 @@ def tile_picked_yqbn_norm_p_kernel(
                 rhs=e_g[:].bitcast(FP8X4), rhs_scale=es_g[E_ROW:P, :], start=True, stop=True,
             )
 
-        def row_max(t):
-            neg_top[t] = sb("neg_top%d" % t, [P, 1], F32)
-            nc.vector.tensor_reduce(neg_top[t][:], y_ps[t][:], AX.X, ALU.max, negate=True)
+        close_h(0)
+        ds_g = sb("ds_g", [P, V], U8, tag="x1_first_then_ds_g")
+        gather(ds_g[:], ds_win, qry_t, 0, V)
+        for t in range(1, TILES):
+            close_h(t)
+        quant_h(0, 1, h_first[:].rearrange("p s c -> p (s c)"))
+        gather(e_g[:], e_win, bank_t, 0, U)
+        bank_scores(0)
+        quant_h(1, TILES - 1, h_rest[:].rearrange("p t s c -> p (t s c)"))
+        for t in range(1, TILES):
+            bank_scores(t)
 
         total = sb("total", [P, TILES], F32)
         inv = sb("inv", [P, TILES], F32)
-
-        def bank_sum(t):
+        for t in range(TILES):
+            neg_top[t] = sb("neg_top%d" % t, [P, 1], F32)
+            nc.vector.tensor_reduce(neg_top[t][:], y_ps[t][:], AX.X, ALU.max, negate=True)
             ex = sb("ex%d" % t, [P, U], F32)
             nc.scalar.activation(ex[:], y_ps[t][:], ACT.Exp, bias=neg_top[t][:], accum_out=total[:, t : t + 1])
 
-        def finish(t):
-            s_ps = psum_h.tile([P, V], F32, name="h_ps")
+        half = V // 2
+        for n in range(2):
+            gather(d_g[:, n * half : (n + 1) * half], d_win, qry_t, n * half, (n + 1) * half)
+        nc.vector.reciprocal(inv[:], total[:])
+        num = [sb("num%d" % t, [P, V], F32) for t in range(TILES)]
+
+        def query_ratio(dst, t, cols, s_ps):
             nc.tensor.matmul_mx(
                 out=s_ps[:], lhsT=h_codes[t].bitcast(FP8X4), lhsT_scale=h_sc[t],
-                rhs=d_g[:].bitcast(FP8X4), rhs_scale=ds_g[D_ROW:P, :], start=True, stop=True,
+                rhs=d_g[:, cols].bitcast(FP8X4), rhs_scale=ds_g[D_ROW:P, cols], start=True, stop=True,
             )
-            num = sb("num%d" % t, [P, V], F32)
-            nc.scalar.activation(num[:], s_ps[:], ACT.Exp, bias=neg_top[t][:])
-            res = sb("res%d" % t, [P, V], F32)
-            nc.vector.tensor_scalar(res[:], num[:], inv[:, t : t + 1], None, ALU.mult)
-            nc.sync.dma_start(out=out[t * P : (t + 1) * P, :], in_=res[:])
+            nc.scalar.activation(num[t][:, cols], s_ps[:], ACT.Exp, bias=neg_top[t][:])
+            nc.vector.tensor_scalar(dst, num[t][:, cols], inv[:, t : t + 1], None, ALU.mult)
 
-        d_g = sb("d_g", [P, V], U32)
-        close_h(0)
-        ds_g = at("ds_g", 0, [P, V], U8)
-        nc.vector.tensor_copy(ds_g[:], ds_win[:].indirect(qry_t[:]))
-        for t in range(1, TILES):
-            close_h(t)
-        quant_h(0, 1, sb("h_codes0", [P, P], U32))
-        nc.vector.tensor_copy(e_g[:], ew_win[:].indirect(bank_t[:]))
-        bank_scores(0)
-        quant_h(1, 3, sb("h_codes1", [P, 3 * P], U32))
-        for t in range(1, TILES):
-            bank_scores(t)
-        row_max(0)
-        bank_sum(0)
-        for t in range(1, TILES):
-            row_max(t)
-            bank_sum(t)
-        nc.vector.tensor_copy(d_g[:], dw_win[:].indirect(qry_t[:]))
-        nc.vector.reciprocal(inv[:], total[:])
-        for t in range(TILES):
-            finish(t)
+        front = out[0 : 2 * P, :].rearrange("(t p) v -> p t v", t=2)
+        for n in range(2):
+            cols = slice(n * half, (n + 1) * half)
+            pair = sb("pair%d" % n, [P, 2, half], F32)
+            for t in range(2):
+                query_ratio(pair[:, t, :], t, cols, psum_h.tile([P, half], F32, name="h_ps"))
+            nc.sync.dma_start(out=front[:, :, cols], in_=pair[:])
+        for t in range(2, TILES):
+            res = sb("res%d" % t, [P, V], F32)
+            query_ratio(res[:], t, slice(0, V), psum_y.tile([P, V], F32, name="y_ps"))
+            nc.sync.dma_start(out=out[t * P : (t + 1) * P, :], in_=res[:])

@@ -55,13 +55,13 @@ def tile_picked_yqbn_norm_p_kernel(
         nc.vector.memset(es_win[:].bitcast(I32), 0)
         nc.vector.memset(ds_win[:].bitcast(I32), 0)
 
-        def load_words(win, words):
-            nc.sync.dma_start(out=win[:].bitcast(I32), in_=words.rearrange("p n t -> p (n t)").bitcast(I32))
+        def load_words(win, words, queue=nc.sync):
+            queue.dma_start(out=win[:].bitcast(I32), in_=words.rearrange("p n t -> p (n t)").bitcast(I32))
 
-        def load_scales(win, row, scales):
+        def load_scales(win, row, scales, queues=(nc.sync,) * 4):
             rows = scales.shape[0] * 4
-            for q in QUADRANTS:
-                nc.sync.dma_start(
+            for q, queue in zip(QUADRANTS, queues):
+                queue.dma_start(
                     out=win[32 * q + row : 32 * q + row + rows, :].bitcast(I32),
                     in_=scales[:, 4 * q : 4 * q + 4, :].bitcast(I32),
                 )
@@ -74,16 +74,15 @@ def tile_picked_yqbn_norm_p_kernel(
         e_win = sb("e_win", [P, W], U32)
         d_win = sb("d_win", [P, G], U32)
         nc.sync.dma_start(offs_t[:], offs)
-        load_words(x_win[0], x_words[0])
+        load_words(x_win[0], x_words[0], nc.scalar)
         load_scales(xs_win, 0, x_scales)
-        nc.sync.dma_start(out=w0_raw[:, 0:2, :], in_=w_rows[0][:, 0:2, :])
-        nc.sync.dma_start(out=w0_raw[:, 2:4, :], in_=w_rows[0][:, 2:4, :])
+        nc.sync.dma_start(out=w0_raw[:], in_=w_rows[0])
         nc.sync.dma_start(bank_t[:], bank)
-        load_scales(es_win, E_ROW, e_scales)
+        load_scales(es_win, E_ROW, e_scales, (nc.gpsimd, nc.sync, nc.sync, nc.sync))
         nc.sync.dma_start(out=w1_left[:], in_=w_rows[1][:, :, 0 : H // 2])
         nc.sync.dma_start(out=w1_right[:], in_=w_rows[1][:, :, H // 2 : H])
         nc.sync.dma_start(qry_t[:], qry)
-        load_scales(ds_win, D_ROW, d_scales)
+        load_scales(ds_win, D_ROW, d_scales, (nc.gpsimd, nc.sync, nc.sync, nc.sync))
         load_words(x_win[1], x_words[1])
         load_words(e_win, e_words[0])
         load_words(d_win, d_words[0])

@@ -94,13 +94,15 @@ def tile_picked_yqbn_norm_p_kernel(
         w_codes = [sb("w_codes%d" % o, [P, H], U32) for o in range(PASSES)]
         w_sc = [sb("w_sc%d" % o, [P, H], U8) for o in range(PASSES)]
 
-        def deal_w(copy, raw, o, m0, m1, raw_first=0):
+        def deal_w(copy, raw, o, m0, m1, c0, c1, raw_first=0):
             src = raw[:, :, PACK * (m0 - raw_first) : PACK * (m1 - raw_first)].rearrange("p j (m c) -> p m j c", c=PACK)
-            copy(w_bf[o][:, :, m0:m1, :].rearrange("p c m j -> p m j c"), src)
+            copy(w_bf[o][:, c0:c1, m0:m1, :].rearrange("p c m j -> p m j c"), src[:, :, :, c0:c1])
 
-        def quant_w(o):
+        def quant_w(o, c0, c1):
             nc.vector.quantize_mx(
-                out=w_codes[o][:].bitcast(FP8X4), scales=w_sc[o][:], in_=w_bf[o][:].rearrange("p c m j -> p (c m j)")
+                out=w_codes[o][:, c0 * P : c1 * P].bitcast(FP8X4),
+                scales=w_sc[o][:, c0 * P : c1 * P],
+                in_=w_bf[o][:, c0:c1].rearrange("p c m j -> p (c m j)"),
             )
 
         h_ps = [psum_h.tile([P, PACK, P], F32, name="h_ps") for t in range(TILES)]
@@ -122,17 +124,21 @@ def tile_picked_yqbn_norm_p_kernel(
         es_g = sb("es_g", [P, U], U8)
         gather(x0_g[:], x_win[0], offs_t, 0, S)
         gather(xs_g[:], xs_win, offs_t, 0, S)
-        deal_w(nc.scalar.copy, w0_raw, 0, 0, SCALAR_QUADS_0)
-        deal_w(nc.vector.tensor_copy, w0_raw, 0, SCALAR_QUADS_0, P)
-        quant_w(0)
+        for c in (0, 2):
+            deal_w(nc.scalar.copy, w0_raw, 0, 0, SCALAR_QUADS_0, c, c + 2)
+            deal_w(nc.vector.tensor_copy, w0_raw, 0, SCALAR_QUADS_0, P, c, c + 2)
+        for c in (0, 2):
+            quant_w(0, c, c + 2)
         gather(es_g[:], es_win, bank_t, 0, U)
         for t in range(TILES):
             project(t, 0, x0_g[:, t * P : (t + 1) * P])
 
-        deal_w(nc.scalar.copy, w1_left, 1, 0, P // 2)
-        deal_w(nc.scalar.copy, w1_right, 1, P // 2, SCALAR_QUADS_1, P // 2)
-        deal_w(nc.vector.tensor_copy, w1_right, 1, SCALAR_QUADS_1, P, P // 2)
-        quant_w(1)
+        deal_w(nc.scalar.copy, w1_left, 1, 0, P // 2, 0, PACK)
+        for c in (0, 2):
+            deal_w(nc.scalar.copy, w1_right, 1, P // 2, SCALAR_QUADS_1, c, c + 2, P // 2)
+            deal_w(nc.vector.tensor_copy, w1_right, 1, SCALAR_QUADS_1, P, c, c + 2, P // 2)
+        for c in (0, 2):
+            quant_w(1, c, c + 2)
         x1_first = sb("x1_first", [P, P], U32, tag="x1_first_then_ds_g")
         x1_second = sb("x1_second", [P, P], U32)
         x1_rest = sb("x1_rest", [P, 2 * P], U32)

@@ -24,8 +24,7 @@ LIST = 16
 E_ROW = 8
 D_ROW = 12
 QUADRANTS = (0, 2, 1, 3)
-SCALAR_QUADS_0 = 48
-SCALAR_QUADS_1 = 96
+SCALAR_QUADS = 84
 
 
 def tile_picked_yqbn_norm_p_kernel(
@@ -67,22 +66,22 @@ def tile_picked_yqbn_norm_p_kernel(
                 )
 
         w_rows = w1.rearrange("(o p j) i -> o p j i", o=PASSES, j=PACK)
-        w0_raw = sb("w0_raw", [P, PACK, H], F32)
-        w1_left = sb("w1_left", [P, PACK, H // 2], F32)
-        w1_right = sb("w1_right", [P, PACK, H // 2], F32)
+        w_left = [sb("w_left%d" % o, [P, PACK, H // 2], F32) for o in range(PASSES)]
+        w_right = [sb("w_right%d" % o, [P, PACK, H // 2], F32) for o in range(PASSES)]
         x_win = [sb("x_win%d" % o, [P, T], U32) for o in range(PASSES)]
         e_win = sb("e_win", [P, W], U32)
         d_win = sb("d_win", [P, G], U32)
         nc.sync.dma_start(offs_t[:], offs)
         load_words(x_win[0], x_words[0], nc.scalar)
         load_scales(xs_win, 0, x_scales)
-        nc.sync.dma_start(out=w0_raw[:], in_=w_rows[0])
+        nc.sync.dma_start(out=w_left[0][:], in_=w_rows[0][:, :, 0 : H // 2])
+        nc.sync.dma_start(out=w_right[0][:], in_=w_rows[0][:, :, H // 2 : H])
         nc.sync.dma_start(bank_t[:], bank)
         load_scales(es_win, E_ROW, e_scales, (nc.gpsimd, nc.sync, nc.sync, nc.sync))
-        nc.sync.dma_start(out=w1_left[:], in_=w_rows[1][:, :, 0 : H // 2])
-        nc.sync.dma_start(out=w1_right[:], in_=w_rows[1][:, :, H // 2 : H])
+        nc.sync.dma_start(out=w_left[1][:], in_=w_rows[1][:, :, 0 : H // 2])
+        nc.sync.dma_start(out=w_right[1][:], in_=w_rows[1][:, :, H // 2 : H])
         nc.sync.dma_start(qry_t[:], qry)
-        load_scales(ds_win, D_ROW, d_scales, (nc.gpsimd, nc.sync, nc.sync, nc.sync))
+        load_scales(ds_win, D_ROW, d_scales, (nc.gpsimd, nc.gpsimd, nc.sync, nc.sync))
         load_words(x_win[1], x_words[1])
         load_words(e_win, e_words[0])
         load_words(d_win, d_words[0])
@@ -105,6 +104,14 @@ def tile_picked_yqbn_norm_p_kernel(
                 in_=w_bf[o][:, c0:c1].rearrange("p c m j -> p (c m j)"),
             )
 
+        def prepare_w(o):
+            deal_w(nc.scalar.copy, w_left[o], o, 0, P // 2, 0, PACK)
+            for c in (0, 2):
+                deal_w(nc.scalar.copy, w_right[o], o, P // 2, SCALAR_QUADS, c, c + 2, P // 2)
+                deal_w(nc.vector.tensor_copy, w_right[o], o, SCALAR_QUADS, P, c, c + 2, P // 2)
+            for c in (0, 2):
+                quant_w(o, c, c + 2)
+
         h_ps = [psum_h.tile([P, PACK, P], F32, name="h_ps") for t in range(TILES)]
 
         def project(t, o, rhs):
@@ -124,21 +131,12 @@ def tile_picked_yqbn_norm_p_kernel(
         es_g = sb("es_g", [P, U], U8)
         gather(x0_g[:], x_win[0], offs_t, 0, S)
         gather(xs_g[:], xs_win, offs_t, 0, S)
-        for c in (0, 2):
-            deal_w(nc.scalar.copy, w0_raw, 0, 0, SCALAR_QUADS_0, c, c + 2)
-            deal_w(nc.vector.tensor_copy, w0_raw, 0, SCALAR_QUADS_0, P, c, c + 2)
-        for c in (0, 2):
-            quant_w(0, c, c + 2)
+        prepare_w(0)
         gather(es_g[:], es_win, bank_t, 0, U)
         for t in range(TILES):
             project(t, 0, x0_g[:, t * P : (t + 1) * P])
 
-        deal_w(nc.scalar.copy, w1_left, 1, 0, P // 2, 0, PACK)
-        for c in (0, 2):
-            deal_w(nc.scalar.copy, w1_right, 1, P // 2, SCALAR_QUADS_1, c, c + 2, P // 2)
-            deal_w(nc.vector.tensor_copy, w1_right, 1, SCALAR_QUADS_1, P, c, c + 2, P // 2)
-        for c in (0, 2):
-            quant_w(1, c, c + 2)
+        prepare_w(1)
         x1_first = sb("x1_first", [P, P], U32, tag="x1_first_then_ds_g")
         x1_second = sb("x1_second", [P, P], U32)
         x1_rest = sb("x1_rest", [P, 2 * P], U32)
@@ -168,12 +166,14 @@ def tile_picked_yqbn_norm_p_kernel(
         e_g = sb("e_g", [P, U], U32)
         d_g = sb("d_g", [P, V], U32)
 
-        def bank_scores(t):
-            y_ps[t] = psum_y.tile([P, U], F32, name="y_ps")
+        def scores(dst, t, words, scales):
             nc.tensor.matmul_mx(
-                out=y_ps[t][:], lhsT=h_codes[t].bitcast(FP8X4), lhsT_scale=h_sc[t],
-                rhs=e_g[:].bitcast(FP8X4), rhs_scale=es_g[E_ROW:P, :], start=True, stop=True,
+                out=dst, lhsT=h_codes[t].bitcast(FP8X4), lhsT_scale=h_sc[t],
+                rhs=words.bitcast(FP8X4), rhs_scale=scales, start=True, stop=True,
             )
+
+        def bank_scores(t, first, last):
+            scores(y_ps[t][:, first:last], t, e_g[:, first:last], es_g[E_ROW:P, first:last])
 
         close_h(0)
         ds_g = sb("ds_g", [P, V], U8, tag="x1_first_then_ds_g")
@@ -181,11 +181,17 @@ def tile_picked_yqbn_norm_p_kernel(
         for t in range(1, TILES):
             close_h(t)
         quant_h(0, 1, h_first[:].rearrange("p s c -> p (s c)"))
-        gather(e_g[:], e_win, bank_t, 0, U)
-        bank_scores(0)
-        quant_h(1, TILES - 1, h_rest[:].rearrange("p t s c -> p (t s c)"))
+        for t in range(TILES):
+            y_ps[t] = psum_y.tile([P, U], F32, name="y_ps")
+        gather(e_g[:, 0 : U - P], e_win, bank_t, 0, U - P)
+        bank_scores(0, 0, 2 * P)
+        bank_scores(0, 2 * P, U - P)
+        gather(e_g[:, U - P : U], e_win, bank_t, U - P, U)
+        bank_scores(0, U - P, U)
+        quant_h(1, 2, h_rest[:, 0:2].rearrange("p t s c -> p (t s c)"))
+        quant_h(3, 1, h_rest[:, 2].rearrange("p s c -> p (s c)"))
         for t in range(1, TILES):
-            bank_scores(t)
+            bank_scores(t, 0, U)
 
         total = sb("total", [P, TILES], F32)
         inv = sb("inv", [P, TILES], F32)
@@ -202,10 +208,7 @@ def tile_picked_yqbn_norm_p_kernel(
         num = [sb("num%d" % t, [P, V], F32) for t in range(TILES)]
 
         def query_ratio(dst, t, cols, s_ps):
-            nc.tensor.matmul_mx(
-                out=s_ps[:], lhsT=h_codes[t].bitcast(FP8X4), lhsT_scale=h_sc[t],
-                rhs=d_g[:, cols].bitcast(FP8X4), rhs_scale=ds_g[D_ROW:P, cols], start=True, stop=True,
-            )
+            scores(s_ps[:], t, d_g[:, cols], ds_g[D_ROW:P, cols])
             nc.scalar.activation(num[t][:, cols], s_ps[:], ACT.Exp, bias=neg_top[t][:])
             nc.vector.tensor_scalar(dst, num[t][:, cols], inv[:, t : t + 1], None, ALU.mult)
 

@@ -24,6 +24,7 @@ LIST = 16
 E_ROW = 8
 D_ROW = 12
 QUADRANTS = (0, 2, 1, 3)
+SPREAD = 8
 SCALAR_QUADS = 84
 
 
@@ -53,16 +54,22 @@ def tile_picked_yqbn_norm_p_kernel(
         nc.scalar.activation(warm_out[:], warm_in[:], ACT.Exp)
         nc.vector.memset(es_win[:].bitcast(I32), 0)
         nc.vector.memset(ds_win[:].bitcast(I32), 0)
+        es_plane = sb("es_plane", [P, U], U8)
+        ds_plane = sb("ds_plane", [P, V], U8)
+        nc.vector.memset(es_plane[:].bitcast(I32), 0)
+        nc.vector.memset(ds_plane[:].bitcast(I32), 0)
 
         def load_words(win, words, queue=nc.sync):
             queue.dma_start(out=win[:].bitcast(I32), in_=words.rearrange("p n t -> p (n t)").bitcast(I32))
 
-        def load_scales(win, row, scales, queues=(nc.sync,) * 4):
-            rows = scales.shape[0] * 4
-            for q, queue in zip(QUADRANTS, queues):
-                queue.dma_start(
-                    out=win[32 * q + row : 32 * q + row + rows, :].bitcast(I32),
-                    in_=scales[:, 4 * q : 4 * q + 4, :].bitcast(I32),
+        def load_spread(win, scales):
+            nc.sync.dma_start(out=win[0:P:SPREAD, :].bitcast(I32), in_=scales[0].bitcast(I32))
+
+        def place_rows(plane, row, picked):
+            for q in QUADRANTS:
+                nc.sync.dma_start(
+                    out=plane[32 * q + row : 32 * q + row + 4, :].bitcast(I32),
+                    in_=picked[32 * q : 32 * q + 32 : SPREAD, :].bitcast(I32),
                 )
 
         w_rows = w1.rearrange("(o p j) i -> o p j i", o=PASSES, j=PACK)
@@ -73,18 +80,21 @@ def tile_picked_yqbn_norm_p_kernel(
         d_win = sb("d_win", [P, G], U32)
         nc.sync.dma_start(offs_t[:], offs)
         load_words(x_win[0], x_words[0], nc.scalar)
-        load_scales(xs_win, 0, x_scales)
+        for q in QUADRANTS:
+            nc.sync.dma_start(
+                out=xs_win[32 * q : 32 * q + 4 * PASSES, :].bitcast(I32),
+                in_=x_scales[:, 4 * q : 4 * q + 4, :].bitcast(I32),
+            )
         nc.sync.dma_start(out=w_left[0][:], in_=w_rows[0][:, :, 0 : H // 2])
         nc.sync.dma_start(out=w_right[0][:], in_=w_rows[0][:, :, H // 2 : H])
         nc.sync.dma_start(bank_t[:], bank)
-        load_scales(es_win, E_ROW, e_scales, (nc.gpsimd, nc.sync, nc.sync, nc.sync))
+        load_spread(es_win, e_scales)
         nc.sync.dma_start(out=w_left[1][:], in_=w_rows[1][:, :, 0 : H // 2])
         nc.sync.dma_start(out=w_right[1][:], in_=w_rows[1][:, :, H // 2 : H])
         nc.sync.dma_start(qry_t[:], qry)
-        load_scales(ds_win, D_ROW, d_scales, (nc.gpsimd, nc.gpsimd, nc.sync, nc.sync))
+        load_spread(ds_win, d_scales)
         load_words(x_win[1], x_words[1])
         load_words(e_win, e_words[0])
-        load_words(d_win, d_words[0])
 
         def gather(dst, win, entries, first, last):
             nc.vector.tensor_copy(dst, win[:].indirect(entries[:, first // LIST : last // LIST]))
@@ -133,6 +143,8 @@ def tile_picked_yqbn_norm_p_kernel(
         gather(xs_g[:], xs_win, offs_t, 0, S)
         prepare_w(0)
         gather(es_g[:], es_win, bank_t, 0, U)
+        place_rows(es_plane, E_ROW, es_g)
+        load_words(d_win, d_words[0])
         for t in range(TILES):
             project(t, 0, x0_g[:, t * P : (t + 1) * P])
 
@@ -173,11 +185,12 @@ def tile_picked_yqbn_norm_p_kernel(
             )
 
         def bank_scores(t, first, last):
-            scores(y_ps[t][:, first:last], t, e_g[:, first:last], es_g[E_ROW:P, first:last])
+            scores(y_ps[t][:, first:last], t, e_g[:, first:last], es_plane[E_ROW:P, first:last])
 
         close_h(0)
         ds_g = sb("ds_g", [P, V], U8, tag="x1_first_then_ds_g")
         gather(ds_g[:], ds_win, qry_t, 0, V)
+        place_rows(ds_plane, D_ROW, ds_g)
         for t in range(1, TILES):
             close_h(t)
         quant_h(0, 1, h_first[:].rearrange("p s c -> p (s c)"))
@@ -208,7 +221,7 @@ def tile_picked_yqbn_norm_p_kernel(
         num = [sb("num%d" % t, [P, V], F32) for t in range(TILES)]
 
         def query_ratio(dst, t, cols, s_ps):
-            scores(s_ps[:], t, d_g[:, cols], ds_g[D_ROW:P, cols])
+            scores(s_ps[:], t, d_g[:, cols], ds_plane[D_ROW:P, cols])
             nc.scalar.activation(num[t][:, cols], s_ps[:], ACT.Exp, bias=neg_top[t][:])
             nc.vector.tensor_scalar(dst, num[t][:, cols], inv[:, t : t + 1], None, ALU.mult)
 

@@ -54,10 +54,6 @@ def tile_picked_yqbn_norm_p_kernel(
         nc.scalar.activation(warm_out[:], warm_in[:], ACT.Exp)
         nc.vector.memset(es_win[:].bitcast(I32), 0)
         nc.vector.memset(ds_win[:].bitcast(I32), 0)
-        es_plane = sb("es_plane", [P, U], U8)
-        ds_plane = sb("ds_plane", [P, V], U8)
-        nc.vector.memset(es_plane[:].bitcast(I32), 0)
-        nc.vector.memset(ds_plane[:].bitcast(I32), 0)
 
         def load_words(win, words, queue=nc.sync):
             queue.dma_start(out=win[:].bitcast(I32), in_=words.rearrange("p n t -> p (n t)").bitcast(I32))
@@ -67,14 +63,14 @@ def tile_picked_yqbn_norm_p_kernel(
 
         def place_rows(plane, row, picked):
             for q in QUADRANTS:
-                nc.sync.dma_start(
+                nc.scalar.dma_start(
                     out=plane[32 * q + row : 32 * q + row + 4, :].bitcast(I32),
                     in_=picked[32 * q : 32 * q + 32 : SPREAD, :].bitcast(I32),
                 )
 
         w_rows = w1.rearrange("(o p j) i -> o p j i", o=PASSES, j=PACK)
         w_left = [sb("w_left%d" % o, [P, PACK, H // 2], F32) for o in range(PASSES)]
-        w_right = [sb("w_right%d" % o, [P, PACK, H // 2], F32) for o in range(PASSES)]
+        w_right = [sb("w_right0", [P, PACK, H // 2], F32), sb("w_right1", [P, PACK, H // 2], F32, tag="w_right1_then_es_plane")]
         x_win = [sb("x_win%d" % o, [P, T], U32) for o in range(PASSES)]
         e_win = sb("e_win", [P, W], U32)
         d_win = sb("d_win", [P, G], U32)
@@ -95,6 +91,7 @@ def tile_picked_yqbn_norm_p_kernel(
         load_spread(ds_win, d_scales)
         load_words(x_win[1], x_words[1])
         load_words(e_win, e_words[0])
+        load_words(d_win, d_words[0])
 
         def gather(dst, win, entries, first, last):
             nc.vector.tensor_copy(dst, win[:].indirect(entries[:, first // LIST : last // LIST]))
@@ -143,12 +140,12 @@ def tile_picked_yqbn_norm_p_kernel(
         gather(xs_g[:], xs_win, offs_t, 0, S)
         prepare_w(0)
         gather(es_g[:], es_win, bank_t, 0, U)
-        place_rows(es_plane, E_ROW, es_g)
-        load_words(d_win, d_words[0])
         for t in range(TILES):
             project(t, 0, x0_g[:, t * P : (t + 1) * P])
 
         prepare_w(1)
+        es_plane = sb("es_plane", [P, U], U8, tag="w_right1_then_es_plane")
+        place_rows(es_plane, E_ROW, es_g)
         x1_first = sb("x1_first", [P, P], U32, tag="x1_first_then_ds_g")
         x1_second = sb("x1_second", [P, P], U32)
         x1_rest = sb("x1_rest", [P, 2 * P], U32)
@@ -190,9 +187,10 @@ def tile_picked_yqbn_norm_p_kernel(
         close_h(0)
         ds_g = sb("ds_g", [P, V], U8, tag="x1_first_then_ds_g")
         gather(ds_g[:], ds_win, qry_t, 0, V)
-        place_rows(ds_plane, D_ROW, ds_g)
         for t in range(1, TILES):
             close_h(t)
+        ds_plane = sb("ds_plane", [P, V], U8)
+        place_rows(ds_plane, D_ROW, ds_g)
         quant_h(0, 1, h_first[:].rearrange("p s c -> p (s c)"))
         for t in range(TILES):
             y_ps[t] = psum_y.tile([P, U], F32, name="y_ps")

@@ -73,7 +73,6 @@ def tile_picked_yqbn_norm_p_kernel(
         w_right = [sb("w_right0", [P, PACK, H // 2], F32), sb("w_right1", [P, PACK, H // 2], F32, tag="w_right1_then_es_plane")]
         x_win = [sb("x_win%d" % o, [P, T], U32) for o in range(PASSES)]
         e_win = sb("e_win", [P, W], U32)
-        d_win = sb("d_win", [P, G], U32)
         nc.sync.dma_start(offs_t[:], offs)
         load_words(x_win[0], x_words[0], nc.scalar)
         for q in QUADRANTS:
@@ -91,7 +90,6 @@ def tile_picked_yqbn_norm_p_kernel(
         load_spread(ds_win, d_scales)
         load_words(x_win[1], x_words[1])
         load_words(e_win, e_words[0])
-        load_words(d_win, d_words[0])
 
         def gather(dst, win, entries, first, last):
             nc.vector.tensor_copy(dst, win[:].indirect(entries[:, first // LIST : last // LIST]))
@@ -135,7 +133,7 @@ def tile_picked_yqbn_norm_p_kernel(
 
         x0_g = sb("x0_g", [P, S], U32)
         xs_g = sb("xs_g", [P, S], U8)
-        es_g = sb("es_g", [P, U], U8)
+        es_g = sb("es_g", [P, U], U8, tag="es_g_then_d_win")
         gather(x0_g[:], x_win[0], offs_t, 0, S)
         gather(xs_g[:], xs_win, offs_t, 0, S)
         prepare_w(0)
@@ -146,6 +144,8 @@ def tile_picked_yqbn_norm_p_kernel(
         prepare_w(1)
         es_plane = sb("es_plane", [P, U], U8, tag="w_right1_then_es_plane")
         place_rows(es_plane, E_ROW, es_g)
+        d_win = sb("d_win", [P, G], U32, tag="es_g_then_d_win")
+        load_words(d_win, d_words[0])
         x1_first = sb("x1_first", [P, P], U32, tag="x1_first_then_ds_g")
         x1_second = sb("x1_second", [P, P], U32)
         x1_rest = sb("x1_rest", [P, 2 * P], U32)

@@ -48,12 +48,12 @@ def tile_picked_yqbn_norm_p_kernel(
         es_win = sb("es_win", [P, W], U8)
         ds_win = sb("ds_win", [P, G], U8)
         nc.vector.memset(xs_win[:].bitcast(I32), 0)
+        nc.vector.memset(es_win[:].bitcast(I32), 0)
+        nc.vector.memset(ds_win[:].bitcast(I32), 0)
         warm_in = sb("warm_in", [P, 8], F32)
         warm_out = sb("warm_out", [P, 8], F32)
         nc.vector.memset(warm_in[:], 0.0)
         nc.scalar.activation(warm_out[:], warm_in[:], ACT.Exp)
-        nc.vector.memset(es_win[:].bitcast(I32), 0)
-        nc.vector.memset(ds_win[:].bitcast(I32), 0)
 
         def load_words(win, words, queue=nc.sync):
             queue.dma_start(out=win[:].bitcast(I32), in_=words.rearrange("p n t -> p (n t)").bitcast(I32))
@@ -63,36 +63,59 @@ def tile_picked_yqbn_norm_p_kernel(
 
         def place_rows(plane, row, picked):
             for q in QUADRANTS:
-                nc.scalar.dma_start(
+                nc.sync.dma_start(
                     out=plane[32 * q + row : 32 * q + row + 4, :].bitcast(I32),
                     in_=picked[32 * q : 32 * q + 32 : SPREAD, :].bitcast(I32),
                 )
 
+        def gather(dst, win, entries, first, last):
+            nc.vector.tensor_copy(dst, win[:].indirect(entries[:, first // LIST : last // LIST]))
+
         w_rows = w1.rearrange("(o p j) i -> o p j i", o=PASSES, j=PACK)
         w_left = [sb("w_left%d" % o, [P, PACK, H // 2], F32) for o in range(PASSES)]
-        w_right = [sb("w_right0", [P, PACK, H // 2], F32), sb("w_right1", [P, PACK, H // 2], F32, tag="w_right1_then_es_plane")]
+        w_right = [sb("w_right%d" % o, [P, PACK, H // 2], F32) for o in range(PASSES)]
         x_win = [sb("x_win%d" % o, [P, T], U32) for o in range(PASSES)]
         e_win = sb("e_win", [P, W], U32)
-        nc.sync.dma_start(offs_t[:], offs)
-        load_words(x_win[0], x_words[0], nc.scalar)
-        for q in QUADRANTS:
-            nc.sync.dma_start(
+        d_win = sb("d_win", [P, G], U32)
+
+        def load_x_scales(queue, q):
+            queue.dma_start(
                 out=xs_win[32 * q : 32 * q + 4 * PASSES, :].bitcast(I32),
                 in_=x_scales[:, 4 * q : 4 * q + 4, :].bitcast(I32),
             )
-        nc.sync.dma_start(out=w_left[0][:], in_=w_rows[0][:, :, 0 : H // 2])
-        nc.sync.dma_start(out=w_right[0][:], in_=w_rows[0][:, :, H // 2 : H])
+
+        def load_w(o):
+            nc.sync.dma_start(out=w_left[o][:], in_=w_rows[o][:, :, 0 : H // 2])
+            nc.sync.dma_start(out=w_right[o][:], in_=w_rows[o][:, :, H // 2 : H])
+
+        nc.sync.dma_start(offs_t[:], offs)
+        load_words(x_win[0], x_words[0], nc.scalar)
+        for q in QUADRANTS[:2]:
+            load_x_scales(nc.gpsimd, q)
         nc.sync.dma_start(bank_t[:], bank)
         load_spread(es_win, e_scales)
-        nc.sync.dma_start(out=w_left[1][:], in_=w_rows[1][:, :, 0 : H // 2])
-        nc.sync.dma_start(out=w_right[1][:], in_=w_rows[1][:, :, H // 2 : H])
         nc.sync.dma_start(qry_t[:], qry)
         load_spread(ds_win, d_scales)
+        load_w(0)
+        for q in QUADRANTS[2:]:
+            load_x_scales(nc.sync, q)
+        load_w(1)
         load_words(x_win[1], x_words[1])
         load_words(e_win, e_words[0])
 
-        def gather(dst, win, entries, first, last):
-            nc.vector.tensor_copy(dst, win[:].indirect(entries[:, first // LIST : last // LIST]))
+        ds_g = sb("ds_g", [P, V], U8)
+        es_g = sb("es_g", [P, U], U8)
+        x0_g = sb("x0_g", [P, S], U32)
+        xs_g = [sb("xs_g%d" % n, [P, S // 2], U8) for n in range(2)]
+        gather(x0_g[:], x_win[0], offs_t, 0, S)
+        gather(es_g[:], es_win, bank_t, 0, U)
+        gather(ds_g[:], ds_win, qry_t, 0, V)
+
+        es_plane = sb("es_plane", [P, U], U8)
+        ds_plane = sb("ds_plane", [P, V], U8)
+        place_rows(es_plane, E_ROW, es_g)
+        load_words(d_win, d_words[0])
+        place_rows(ds_plane, D_ROW, ds_g)
 
         w_bf = [sb("w_bf%d" % o, [P, PACK, P, PACK], BF16) for o in range(PASSES)]
         w_codes = [sb("w_codes%d" % o, [P, H], U32) for o in range(PASSES)]
@@ -126,27 +149,19 @@ def tile_picked_yqbn_norm_p_kernel(
                     lhsT=w_codes[o][:, c * P : (c + 1) * P].bitcast(FP8X4),
                     lhsT_scale=w_sc[o][:, c * P : (c + 1) * P],
                     rhs=rhs.bitcast(FP8X4),
-                    rhs_scale=xs_g[4 * o : P, t * P : (t + 1) * P],
+                    rhs_scale=xs_g[t // 2][4 * o : P, t % 2 * P : (t % 2 + 1) * P],
                     start=(o == 0 and c == 0),
                     stop=(o == PASSES - 1 and c == PACK - 1),
                 )
 
-        x0_g = sb("x0_g", [P, S], U32)
-        xs_g = sb("xs_g", [P, S], U8)
-        es_g = sb("es_g", [P, U], U8, tag="es_g_then_d_win")
-        gather(x0_g[:], x_win[0], offs_t, 0, S)
-        gather(xs_g[:], xs_win, offs_t, 0, S)
         prepare_w(0)
-        gather(es_g[:], es_win, bank_t, 0, U)
+        for n in range(2):
+            gather(xs_g[n][:], xs_win, offs_t, n * S // 2, (n + 1) * S // 2)
         for t in range(TILES):
             project(t, 0, x0_g[:, t * P : (t + 1) * P])
 
         prepare_w(1)
-        es_plane = sb("es_plane", [P, U], U8, tag="w_right1_then_es_plane")
-        place_rows(es_plane, E_ROW, es_g)
-        d_win = sb("d_win", [P, G], U32, tag="es_g_then_d_win")
-        load_words(d_win, d_words[0])
-        x1_first = sb("x1_first", [P, P], U32, tag="x1_first_then_ds_g")
+        x1_first = sb("x1_first", [P, P], U32)
         x1_second = sb("x1_second", [P, P], U32)
         x1_rest = sb("x1_rest", [P, 2 * P], U32)
         gather(x1_first[:], x_win[1], offs_t, 0, P)
@@ -157,8 +172,7 @@ def tile_picked_yqbn_norm_p_kernel(
         h_first = sb("h_first", [P, P, PACK], BF16)
         h_rest = sb("h_rest", [P, TILES - 1, P, PACK], BF16)
         h_bf = [h_first[:]] + [h_rest[:, t - 1] for t in range(1, TILES)]
-
-        def close_h(t):
+        for t in range(TILES):
             project(t, 1, x1_g[t])
             nc.scalar.copy(h_bf[t], h_ps[t][:].rearrange("p c s -> p s c"))
 
@@ -184,13 +198,6 @@ def tile_picked_yqbn_norm_p_kernel(
         def bank_scores(t, first, last):
             scores(y_ps[t][:, first:last], t, e_g[:, first:last], es_plane[E_ROW:P, first:last])
 
-        close_h(0)
-        ds_g = sb("ds_g", [P, V], U8, tag="x1_first_then_ds_g")
-        gather(ds_g[:], ds_win, qry_t, 0, V)
-        for t in range(1, TILES):
-            close_h(t)
-        ds_plane = sb("ds_plane", [P, V], U8)
-        place_rows(ds_plane, D_ROW, ds_g)
         quant_h(0, 1, h_first[:].rearrange("p s c -> p (s c)"))
         for t in range(TILES):
             y_ps[t] = psum_y.tile([P, U], F32, name="y_ps")

@@ -25,6 +25,7 @@ E_ROW = 8
 D_ROW = 12
 QUADRANTS = (0, 2, 1, 3)
 SPREAD = 8
+LAST = P - 16
 SCALAR_QUADS = 84
 
 
@@ -48,7 +49,7 @@ def tile_picked_yqbn_norm_p_kernel(
         es_win = sb("es_win", [P, W], U8)
         ds_win = sb("ds_win", [P, G], U8)
         nc.vector.memset(xs_win[:].bitcast(I32), 0)
-        nc.vector.memset(es_win[:].bitcast(I32), 0)
+        nc.vector.memset(es_win[0:LAST, :].bitcast(I32), 0)
         nc.vector.memset(ds_win[:].bitcast(I32), 0)
         warm_in = sb("warm_in", [P, 8], F32)
         warm_out = sb("warm_out", [P, 8], F32)
@@ -61,11 +62,11 @@ def tile_picked_yqbn_norm_p_kernel(
         def load_spread(win, scales):
             nc.sync.dma_start(out=win[0:P:SPREAD, :].bitcast(I32), in_=scales[0].bitcast(I32))
 
-        def place_rows(plane, row, picked):
+        def place_rows(plane, row, picked, first, step):
             for q in QUADRANTS:
                 nc.sync.dma_start(
                     out=plane[32 * q + row : 32 * q + row + 4, :].bitcast(I32),
-                    in_=picked[32 * q : 32 * q + 32 : SPREAD, :].bitcast(I32),
+                    in_=picked[first + 4 * q * step : first + 4 * (q + 1) * step : step, :].bitcast(I32),
                 )
 
         def gather(dst, win, entries, first, last):
@@ -88,17 +89,15 @@ def tile_picked_yqbn_norm_p_kernel(
             nc.sync.dma_start(out=w_left[o][:], in_=w_rows[o][:, :, 0 : H // 2])
             nc.sync.dma_start(out=w_right[o][:], in_=w_rows[o][:, :, H // 2 : H])
 
-        nc.sync.dma_start(offs_t[:], offs)
-        load_words(x_win[0], x_words[0], nc.scalar)
-        for q in QUADRANTS[:2]:
-            load_x_scales(nc.gpsimd, q)
+        nc.scalar.dma_start(out=es_win[LAST:P, :].bitcast(I32), in_=e_scales[0].bitcast(I32))
         nc.sync.dma_start(bank_t[:], bank)
-        load_spread(es_win, e_scales)
+        nc.sync.dma_start(offs_t[:], offs)
+        load_words(x_win[0], x_words[0])
+        for q in QUADRANTS:
+            load_x_scales(nc.sync, q)
         nc.sync.dma_start(qry_t[:], qry)
         load_spread(ds_win, d_scales)
         load_w(0)
-        for q in QUADRANTS[2:]:
-            load_x_scales(nc.sync, q)
         load_w(1)
         load_words(x_win[1], x_words[1])
         load_words(e_win, e_words[0])
@@ -106,16 +105,17 @@ def tile_picked_yqbn_norm_p_kernel(
         ds_g = sb("ds_g", [P, V], U8)
         es_g = sb("es_g", [P, U], U8)
         x0_g = sb("x0_g", [P, S], U32)
-        xs_g = [sb("xs_g%d" % n, [P, S // 2], U8) for n in range(2)]
-        gather(x0_g[:], x_win[0], offs_t, 0, S)
+        xs_g = sb("xs_g", [P, S], U8)
         gather(es_g[:], es_win, bank_t, 0, U)
+        gather(x0_g[:], x_win[0], offs_t, 0, S)
+        gather(xs_g[:], xs_win, offs_t, 0, S)
         gather(ds_g[:], ds_win, qry_t, 0, V)
 
         es_plane = sb("es_plane", [P, U], U8)
         ds_plane = sb("ds_plane", [P, V], U8)
-        place_rows(es_plane, E_ROW, es_g)
+        place_rows(es_plane, E_ROW, es_g, LAST, 1)
         load_words(d_win, d_words[0])
-        place_rows(ds_plane, D_ROW, ds_g)
+        place_rows(ds_plane, D_ROW, ds_g, 0, SPREAD)
 
         w_bf = [sb("w_bf%d" % o, [P, PACK, P, PACK], BF16) for o in range(PASSES)]
         w_codes = [sb("w_codes%d" % o, [P, H], U32) for o in range(PASSES)]
@@ -149,14 +149,12 @@ def tile_picked_yqbn_norm_p_kernel(
                     lhsT=w_codes[o][:, c * P : (c + 1) * P].bitcast(FP8X4),
                     lhsT_scale=w_sc[o][:, c * P : (c + 1) * P],
                     rhs=rhs.bitcast(FP8X4),
-                    rhs_scale=xs_g[t // 2][4 * o : P, t % 2 * P : (t % 2 + 1) * P],
+                    rhs_scale=xs_g[4 * o : P, t * P : (t + 1) * P],
                     start=(o == 0 and c == 0),
                     stop=(o == PASSES - 1 and c == PACK - 1),
                 )
 
         prepare_w(0)
-        for n in range(2):
-            gather(xs_g[n][:], xs_win, offs_t, n * S // 2, (n + 1) * S // 2)
         for t in range(TILES):
             project(t, 0, x0_g[:, t * P : (t + 1) * P])
 

@@ -89,15 +89,15 @@ def tile_picked_yqbn_norm_p_kernel(
             nc.sync.dma_start(out=w_left[o][:], in_=w_rows[o][:, :, 0 : H // 2])
             nc.sync.dma_start(out=w_right[o][:], in_=w_rows[o][:, :, H // 2 : H])
 
-        nc.scalar.dma_start(out=es_win[LAST:P, :].bitcast(I32), in_=e_scales[0].bitcast(I32))
         nc.sync.dma_start(bank_t[:], bank)
-        nc.sync.dma_start(offs_t[:], offs)
+        nc.sync.dma_start(out=es_win[LAST:P, :].bitcast(I32), in_=e_scales[0].bitcast(I32))
         load_words(x_win[0], x_words[0])
+        nc.sync.dma_start(offs_t[:], offs)
         for q in QUADRANTS:
             load_x_scales(nc.sync, q)
+        load_w(0)
         nc.sync.dma_start(qry_t[:], qry)
         load_spread(ds_win, d_scales)
-        load_w(0)
         load_w(1)
         load_words(x_win[1], x_words[1])
         load_words(e_win, e_words[0])
@@ -109,13 +109,11 @@ def tile_picked_yqbn_norm_p_kernel(
         gather(es_g[:], es_win, bank_t, 0, U)
         gather(x0_g[:], x_win[0], offs_t, 0, S)
         gather(xs_g[:], xs_win, offs_t, 0, S)
-        gather(ds_g[:], ds_win, qry_t, 0, V)
 
         es_plane = sb("es_plane", [P, U], U8)
         ds_plane = sb("ds_plane", [P, V], U8)
         place_rows(es_plane, E_ROW, es_g, LAST, 1)
         load_words(d_win, d_words[0])
-        place_rows(ds_plane, D_ROW, ds_g, 0, SPREAD)
 
         w_bf = [sb("w_bf%d" % o, [P, PACK, P, PACK], BF16) for o in range(PASSES)]
         w_codes = [sb("w_codes%d" % o, [P, H], U32) for o in range(PASSES)]
@@ -155,6 +153,8 @@ def tile_picked_yqbn_norm_p_kernel(
                 )
 
         prepare_w(0)
+        gather(ds_g[:], ds_win, qry_t, 0, V)
+        place_rows(ds_plane, D_ROW, ds_g, 0, SPREAD)
         for t in range(TILES):
             project(t, 0, x0_g[:, t * P : (t + 1) * P])
 

@@ -26,7 +26,8 @@ D_ROW = 12
 QUADRANTS = (0, 2, 1, 3)
 SPREAD = 8
 LAST = P - 16
-SCALAR_QUADS = 84
+SCALAR_QUADS_0 = 44
+SCALAR_QUADS_1 = 84
 
 
 def tile_picked_yqbn_norm_p_kernel(
@@ -73,8 +74,9 @@ def tile_picked_yqbn_norm_p_kernel(
             nc.vector.tensor_copy(dst, win[:].indirect(entries[:, first // LIST : last // LIST]))
 
         w_rows = w1.rearrange("(o p j) i -> o p j i", o=PASSES, j=PACK)
-        w_left = [sb("w_left%d" % o, [P, PACK, H // 2], F32) for o in range(PASSES)]
-        w_right = [sb("w_right%d" % o, [P, PACK, H // 2], F32) for o in range(PASSES)]
+        w_whole = sb("w_whole", [P, PACK, H], F32)
+        w_left = sb("w_left", [P, PACK, H // 2], F32)
+        w_right = sb("w_right", [P, PACK, H // 2], F32)
         x_win = [sb("x_win%d" % o, [P, T], U32) for o in range(PASSES)]
         e_win = sb("e_win", [P, W], U32)
         d_win = sb("d_win", [P, G], U32)
@@ -85,20 +87,17 @@ def tile_picked_yqbn_norm_p_kernel(
                 in_=x_scales[:, 4 * q : 4 * q + 4, :].bitcast(I32),
             )
 
-        def load_w(o):
-            nc.sync.dma_start(out=w_left[o][:], in_=w_rows[o][:, :, 0 : H // 2])
-            nc.sync.dma_start(out=w_right[o][:], in_=w_rows[o][:, :, H // 2 : H])
-
         nc.sync.dma_start(bank_t[:], bank)
         nc.sync.dma_start(out=es_win[LAST:P, :].bitcast(I32), in_=e_scales[0].bitcast(I32))
         load_words(x_win[0], x_words[0])
         nc.sync.dma_start(offs_t[:], offs)
         for q in QUADRANTS:
             load_x_scales(nc.sync, q)
-        load_w(0)
+        nc.sync.dma_start(out=w_whole[:], in_=w_rows[0])
         nc.sync.dma_start(qry_t[:], qry)
         load_spread(ds_win, d_scales)
-        load_w(1)
+        nc.sync.dma_start(out=w_left[:], in_=w_rows[1][:, :, 0 : H // 2])
+        nc.sync.dma_start(out=w_right[:], in_=w_rows[1][:, :, H // 2 : H])
         load_words(x_win[1], x_words[1])
         load_words(e_win, e_words[0])
 
@@ -130,11 +129,10 @@ def tile_picked_yqbn_norm_p_kernel(
                 in_=w_bf[o][:, c0:c1].rearrange("p c m j -> p (c m j)"),
             )
 
-        def prepare_w(o):
-            deal_w(nc.scalar.copy, w_left[o], o, 0, P // 2, 0, PACK)
+        def prepare_w(o, last, first_quad, scalar_quads):
             for c in (0, 2):
-                deal_w(nc.scalar.copy, w_right[o], o, P // 2, SCALAR_QUADS, c, c + 2, P // 2)
-                deal_w(nc.vector.tensor_copy, w_right[o], o, SCALAR_QUADS, P, c, c + 2, P // 2)
+                deal_w(nc.scalar.copy, last, o, first_quad, scalar_quads, c, c + 2, first_quad)
+                deal_w(nc.vector.tensor_copy, last, o, scalar_quads, P, c, c + 2, first_quad)
             for c in (0, 2):
                 quant_w(o, c, c + 2)
 
@@ -152,13 +150,14 @@ def tile_picked_yqbn_norm_p_kernel(
                     stop=(o == PASSES - 1 and c == PACK - 1),
                 )
 
-        prepare_w(0)
+        prepare_w(0, w_whole, 0, SCALAR_QUADS_0)
         gather(ds_g[:], ds_win, qry_t, 0, V)
         place_rows(ds_plane, D_ROW, ds_g, 0, SPREAD)
         for t in range(TILES):
             project(t, 0, x0_g[:, t * P : (t + 1) * P])
 
-        prepare_w(1)
+        deal_w(nc.scalar.copy, w_left, 1, 0, P // 2, 0, PACK)
+        prepare_w(1, w_right, P // 2, SCALAR_QUADS_1)
         x1_first = sb("x1_first", [P, P], U32)
         x1_second = sb("x1_second", [P, P], U32)
         x1_rest = sb("x1_rest", [P, 2 * P], U32)

from contextlib import ExitStack

import concourse.mybir as mybir

K, T, S, H, V, W, G, U = 1024, 1024, 512, 512, 256, 2048, 1024, 512
FLOPS = 2 * (K * H * S + H * S * V + H * S * U)

F32 = mybir.dt.float32
BF16 = mybir.dt.bfloat16
I32 = mybir.dt.int32
U32 = mybir.dt.uint32
U16 = mybir.dt.uint16
U8 = mybir.dt.uint8
FP8X4 = mybir.dt.float8_e4m3fn_x4
ACT = mybir.ActivationFunctionType
ALU = mybir.AluOpType
AX = mybir.AxisListType

P = 128
PACK = 4
PASSES = K // (P * PACK)
TILES = S // P
LIST = 16
E_ROW = 8
D_ROW = 12
QUADRANTS = (0, 2, 1, 3)
SPREAD = 8
LAST = P - 16
SCALAR_QUADS_0 = 44
SCALAR_QUADS_1 = 84


def tile_picked_yqbn_norm_p_kernel(
    tc, x_words, x_scales, w1, e_words, e_scales, d_words, d_scales, offs, bank, qry, out
):
    nc = tc.nc
    with ExitStack() as ctx:
        keep = ctx.enter_context(tc.tile_pool(name="keep", bufs=1))
        psum_h = ctx.enter_context(tc.psum_pool(name="psum_h", bufs=TILES))
        psum_y = ctx.enter_context(tc.psum_pool(name="psum_y", bufs=TILES))

        def sb(name, shape, dtype, tag=None):
            return keep.tile(shape, dtype, name=name, tag=tag or name, align_bytes=64)

        offs_t = sb("offs_t", [P, S // LIST], U16)
        bank_t = sb("bank_t", [P, U // LIST], U16)
        qry_t = sb("qry_t", [P, V // LIST], U16)

        xs_win = sb("xs_win", [P, T], U8)
        es_win = sb("es_win", [P, W], U8)
        ds_win = sb("ds_win", [P, G], U8)
        nc.vector.memset(xs_win[:].bitcast(I32), 0)
        nc.vector.memset(es_win[0:LAST, :].bitcast(I32), 0)
        nc.vector.memset(ds_win[:].bitcast(I32), 0)
        warm_in = sb("warm_in", [P, 8], F32)
        warm_out = sb("warm_out", [P, 8], F32)
        nc.vector.memset(warm_in[:], 0.0)
        nc.scalar.activation(warm_out[:], warm_in[:], ACT.Exp)

        def load_words(win, words, queue=nc.sync):
            queue.dma_start(out=win[:].bitcast(I32), in_=words.rearrange("p n t -> p (n t)").bitcast(I32))

        def load_spread(win, scales):
            nc.sync.dma_start(out=win[0:P:SPREAD, :].bitcast(I32), in_=scales[0].bitcast(I32))

        def place_rows(plane, row, picked, first, step):
            for q in QUADRANTS:
                nc.sync.dma_start(
                    out=plane[32 * q + row : 32 * q + row + 4, :].bitcast(I32),
                    in_=picked[first + 4 * q * step : first + 4 * (q + 1) * step : step, :].bitcast(I32),
                )

        def gather(dst, win, entries, first, last):
            nc.vector.tensor_copy(dst, win[:].indirect(entries[:, first // LIST : last // LIST]))

        w_rows = w1.rearrange("(o p j) i -> o p j i", o=PASSES, j=PACK)
        w_whole = sb("w_whole", [P, PACK, H], F32)
        w_left = sb("w_left", [P, PACK, H // 2], F32)
        w_right = sb("w_right", [P, PACK, H // 2], F32)
        x_win = [sb("x_win%d" % o, [P, T], U32) for o in range(PASSES)]
        e_win = sb("e_win", [P, W], U32)
        d_win = sb("d_win", [P, G], U32)

        def load_x_scales(queue, q):
            queue.dma_start(
                out=xs_win[32 * q : 32 * q + 4 * PASSES, :].bitcast(I32),
                in_=x_scales[:, 4 * q : 4 * q + 4, :].bitcast(I32),
            )

        nc.sync.dma_start(bank_t[:], bank)
        nc.sync.dma_start(out=es_win[LAST:P, :].bitcast(I32), in_=e_scales[0].bitcast(I32))
        load_words(x_win[0], x_words[0])
        nc.sync.dma_start(offs_t[:], offs)
        for q in QUADRANTS:
            load_x_scales(nc.sync, q)
        nc.sync.dma_start(out=w_whole[:], in_=w_rows[0])
        nc.sync.dma_start(qry_t[:], qry)
        load_spread(ds_win, d_scales)
        nc.sync.dma_start(out=w_left[:], in_=w_rows[1][:, :, 0 : H // 2])
        nc.sync.dma_start(out=w_right[:], in_=w_rows[1][:, :, H // 2 : H])
        load_words(x_win[1], x_words[1])
        load_words(e_win, e_words[0])

        ds_g = sb("ds_g", [P, V], U8)
        es_g = sb("es_g", [P, U], U8)
        x0_g = sb("x0_g", [P, S], U32)
        xs_g = sb("xs_g", [P, S], U8)
        gather(es_g[:], es_win, bank_t, 0, U)
        gather(x0_g[:], x_win[0], offs_t, 0, S)
        gather(xs_g[:], xs_win, offs_t, 0, S)

        es_plane = sb("es_plane", [P, U], U8)
        ds_plane = sb("ds_plane", [P, V], U8)
        place_rows(es_plane, E_ROW, es_g, LAST, 1)
        load_words(d_win, d_words[0])

        w_bf = [sb("w_bf%d" % o, [P, PACK, P, PACK], BF16) for o in range(PASSES)]
        w_codes = [sb("w_codes%d" % o, [P, H], U32) for o in range(PASSES)]
        w_sc = [sb("w_sc%d" % o, [P, H], U8) for o in range(PASSES)]

        def deal_w(copy, raw, o, m0, m1, c0, c1, raw_first=0):
            src = raw[:, :, PACK * (m0 - raw_first) : PACK * (m1 - raw_first)].rearrange("p j (m c) -> p m j c", c=PACK)
            copy(w_bf[o][:, c0:c1, m0:m1, :].rearrange("p c m j -> p m j c"), src[:, :, :, c0:c1])

        def quant_w(o, c0, c1):
            nc.vector.quantize_mx(
                out=w_codes[o][:, c0 * P : c1 * P].bitcast(FP8X4),
                scales=w_sc[o][:, c0 * P : c1 * P],
                in_=w_bf[o][:, c0:c1].rearrange("p c m j -> p (c m j)"),
            )

        def prepare_w(o, last, first_quad, scalar_quads):
            for c in (0, 2):
                deal_w(nc.scalar.copy, last, o, first_quad, scalar_quads, c, c + 2, first_quad)
                deal_w(nc.vector.tensor_copy, last, o, scalar_quads, P, c, c + 2, first_quad)
            for c in (0, 2):
                quant_w(o, c, c + 2)

        h_ps = [psum_h.tile([P, PACK, P], F32, name="h_ps") for t in range(TILES)]

        def project(t, o, rhs):
            for c in range(PACK):
                nc.tensor.matmul_mx(
                    out=h_ps[t][:, c, :],
                    lhsT=w_codes[o][:, c * P : (c + 1) * P].bitcast(FP8X4),
                    lhsT_scale=w_sc[o][:, c * P : (c + 1) * P],
                    rhs=rhs.bitcast(FP8X4),
                    rhs_scale=xs_g[4 * o : P, t * P : (t + 1) * P],
                    start=(o == 0 and c == 0),
                    stop=(o == PASSES - 1 and c == PACK - 1),
                )

        prepare_w(0, w_whole, 0, SCALAR_QUADS_0)
        gather(ds_g[:], ds_win, qry_t, 0, V)
        place_rows(ds_plane, D_ROW, ds_g, 0, SPREAD)
        for t in range(TILES):
            project(t, 0, x0_g[:, t * P : (t + 1) * P])

        deal_w(nc.scalar.copy, w_left, 1, 0, P // 2, 0, PACK)
        prepare_w(1, w_right, P // 2, SCALAR_QUADS_1)
        x1_first = sb("x1_first", [P, P], U32)
        x1_second = sb("x1_second", [P, P], U32)
        x1_rest = sb("x1_rest", [P, 2 * P], U32)
        gather(x1_first[:], x_win[1], offs_t, 0, P)
        gather(x1_second[:], x_win[1], offs_t, P, 2 * P)
        gather(x1_rest[:], x_win[1], offs_t, 2 * P, S)
        x1_g = [x1_first[:], x1_second[:], x1_rest[:, 0:P], x1_rest[:, P : 2 * P]]

        h_first = sb("h_first", [P, P, PACK], BF16)
        h_rest = sb("h_rest", [P, TILES - 1, P, PACK], BF16)
        h_bf = [h_first[:]] + [h_rest[:, t - 1] for t in range(1, TILES)]
        for t in range(TILES):
            project(t, 1, x1_g[t])
            nc.scalar.copy(h_bf[t], h_ps[t][:].rearrange("p c s -> p s c"))

        h_codes, h_sc, y_ps, neg_top = {}, {}, {}, {}

        def quant_h(first, count, values):
            codes = sb("h_codes%d" % first, [P, count * P], U32)
            scales = sb("h_sc%d" % first, [P, count * P], U8)
            nc.vector.quantize_mx(out=codes[:].bitcast(FP8X4), scales=scales[:], in_=values)
            for n in range(count):
                h_codes[first + n] = codes[:, n * P : (n + 1) * P]
                h_sc[first + n] = scales[:, n * P : (n + 1) * P]

        e_g = sb("e_g", [P, U], U32)
        d_g = sb("d_g", [P, V], U32)

        def scores(dst, t, words, scales):
            nc.tensor.matmul_mx(
                out=dst, lhsT=h_codes[t].bitcast(FP8X4), lhsT_scale=h_sc[t],
                rhs=words.bitcast(FP8X4), rhs_scale=scales, start=True, stop=True,
            )

        def bank_scores(t, first, last):
            scores(y_ps[t][:, first:last], t, e_g[:, first:last], es_plane[E_ROW:P, first:last])

        quant_h(0, 1, h_first[:].rearrange("p s c -> p (s c)"))
        for t in range(TILES):
            y_ps[t] = psum_y.tile([P, U], F32, name="y_ps")
        gather(e_g[:, 0 : U - P], e_win, bank_t, 0, U - P)
        bank_scores(0, 0, 2 * P)
        bank_scores(0, 2 * P, U - P)
        gather(e_g[:, U - P : U], e_win, bank_t, U - P, U)
        bank_scores(0, U - P, U)
        quant_h(1, 2, h_rest[:, 0:2].rearrange("p t s c -> p (t s c)"))
        quant_h(3, 1, h_rest[:, 2].rearrange("p s c -> p (s c)"))
        for t in range(1, TILES):
            bank_scores(t, 0, U)

        total = sb("total", [P, TILES], F32)
        inv = sb("inv", [P, TILES], F32)
        for t in range(TILES):
            neg_top[t] = sb("neg_top%d" % t, [P, 1], F32)
            nc.vector.tensor_reduce(neg_top[t][:], y_ps[t][:], AX.X, ALU.max, negate=True)
            ex = sb("ex%d" % t, [P, U], F32)
            nc.scalar.activation(ex[:], y_ps[t][:], ACT.Exp, bias=neg_top[t][:], accum_out=total[:, t : t + 1])

        half = V // 2
        for n in range(2):
            gather(d_g[:, n * half : (n + 1) * half], d_win, qry_t, n * half, (n + 1) * half)
        nc.vector.reciprocal(inv[:], total[:])
        num = [sb("num%d" % t, [P, V], F32) for t in range(TILES)]

        def query_ratio(dst, t, cols, s_ps):
            scores(s_ps[:], t, d_g[:, cols], ds_plane[D_ROW:P, cols])
            nc.scalar.activation(num[t][:, cols], s_ps[:], ACT.Exp, bias=neg_top[t][:])
            nc.vector.tensor_scalar(dst, num[t][:, cols], inv[:, t : t + 1], None, ALU.mult)

        front = out[0 : 2 * P, :].rearrange("(t p) v -> p t v", t=2)
        for n in range(2):
            cols = slice(n * half, (n + 1) * half)
            pair = sb("pair%d" % n, [P, 2, half], F32)
            for t in range(2):
                query_ratio(pair[:, t, :], t, cols, psum_h.tile([P, half], F32, name="h_ps"))
            nc.sync.dma_start(out=front[:, :, cols], in_=pair[:])
        for t in range(2, TILES):
            res = sb("res%d" % t, [P, V], F32)
            query_ratio(res[:], t, slice(0, V), psum_y.tile([P, V], F32, name="y_ps"))
            nc.sync.dma_start(out=out[t * P : (t + 1) * P, :], in_=res[:])
